import numpy as np, ml_dtypes
CORES = [24,25,26,27,28,29,30,31]
N = 8
import mx_ref
BF = ml_dtypes.bfloat16
def gentries(a):
    return np.ascontiguousarray(a.reshape(8, 16, -1).transpose(0, 2, 1)).reshape(8, -1)
def gtable(e):
    e = np.asarray(e); return np.ascontiguousarray(e.reshape(8, -1, 16).transpose(0, 2, 1)).reshape(128, -1).astype(np.int32)
def gcols(t, e):
    v = np.concatenate([t.reshape(8, 16, -1, 4), np.zeros((8, 16, 1, 4), BF)], axis=2)
    return np.ascontiguousarray(np.stack([v[g][:, e[g]] for g in range(8)])).reshape(128, -1)
def tile(rs):
    return np.stack(rs, axis=2).reshape(128, -1).astype(BF)
def pick(q, e):
    c = np.concatenate([q[0].reshape(128, -1, 4), np.zeros((128, 1, 4), np.uint8)], axis=1); s = np.concatenate([q[1], np.ones((16, 1), np.uint8)], axis=1)
    return (np.ascontiguousarray(c[:, e].reshape(128, -1)), np.ascontiguousarray(s[:, e]))
def join(*qs):
    return (np.concatenate([q[0] for q in qs], axis=1), np.concatenate([q[1] for q in qs], axis=1))
def put(q, e, v):
    c, s = q[0].reshape(128, -1, 4).copy(), q[1].copy(); c[:, e] = v[0].reshape(128, -1, 4); s[:, e] = v[1]
    return (c.reshape(128, -1), s)
def pk(c, s):
    return (np.ascontiguousarray(c), mx_ref.live(s))
def emit(q):
    return q[0], q[1]
def packed(v, rng):
    q = [mx_ref.quantize(np.ascontiguousarray(v[r])) for r in range(N)]
    return np.stack([a for a, b in q]), np.stack([mx_ref.plane(b, rng) for a, b in q])
def values_of_codes():
    e, c = np.zeros((128, 128, 4), np.float32), np.zeros((128, 2, 4), np.uint8)
    e[np.arange(128), np.arange(128), 0] = 1
    c[:127, :, 0] = np.arange(256).reshape(2, 128).T[:127]
    return mx_ref.matmul(mx_ref.quantize(e.reshape(128, 512).astype(BF)), (c.reshape(128, 8), np.full((16, 2), 127, np.uint8))).T.reshape(-1).astype(np.float64)
CODE_VALUE, SCALE_VALUE = values_of_codes(), 2.0 ** (np.arange(256) - 127.0)
def decode(q):
    return (CODE_VALUE[q[0]].reshape(16, 8, -1, 4) * SCALE_VALUE[q[1]][:, None, :, None] + 0.0).reshape(128, -1).astype(np.float32)
def f(rng, *shape):
    return mx_ref.flush((rng.standard_normal(shape, dtype=np.float32) * np.exp2(rng.integers(-2, 3, shape[:-1] + (1,)))).astype(BF))
def wide(rng, *shape, cols=0):
    v = rng.standard_normal(shape, dtype=np.float32) * np.exp2(rng.integers(-12, 13, shape)).astype(np.float32)
    if cols: v *= np.repeat(np.exp2(rng.integers(-cols, cols + 1, shape[:-2] + (1, shape[-1] // 4))) * (rng.random(shape[:-2] + (1, shape[-1] // 4)) > 0.0625), 4, axis=-1).astype(np.float32)
    return mx_ref.flush(v.astype(BF))
C, S, R, SWEEPS = 256, 128, 3, 8
def big(v):
    v = v.astype(np.float32)
    v[np.abs(v) < np.float32(2.0 ** -16)] = 0
    return v
def numbers_of(rng):
    return big(f(rng, N, 128, 4 * C)).reshape(N, 8, 16, C, 4), f(rng, N, 128, 512).astype(np.float32).reshape(N, 128, 128, 4), f(rng, N, 128, 512).astype(np.float32)
def ring(rng, e):
    s, i, n = rng.permutation(C), np.arange(C), np.zeros((3, C), np.int64)
    n[0, s] = s[i ^ 1]
    n[1, s] = s[(((i + 1) ^ 1) - 1) % C]
    n[2, s[e]] = s[e[i ^ 1]]
    return n[rng.permutation(3)], s
def beside(a, b):
    return (a - b) % C in (1, C - 1)
def chords(rng):
    e = rng.permutation(C)
    for i in range(0, C, 2):
        if beside(e[i], e[i + 1]):
            for j in range(0, C, 2):
                if j != i and not beside(e[i], e[j + 1]) and not beside(e[j], e[i + 1]):
                    e[i + 1], e[j + 1] = e[j + 1], e[i + 1]
                    break
    return e
def opposite():
    i = np.arange(S)
    return np.stack([i, i + S], axis=1).reshape(-1)
def crossed(rng):
    i = 2 * np.arange(S)
    return np.stack([i, (i + 2 * rng.integers(1, S - 1) + 1) % C], axis=1).reshape(-1)
def fours(rng):
    s, i, n = rng.permutation(C), np.arange(C), np.zeros((3, C), np.int64)
    for k in range(3): n[k, s] = s[i ^ (k + 1)]
    return n
def graphs(rng):
    return np.stack([np.stack([ring(rng, chords(rng))[0] for g in range(8)]) for r in range(N)])
def layers(rng, still=()):
    w = (big(f(rng, N, 128, 2048)) * np.float32(0.03125)).reshape(N, 128, 512, 4)
    w *= np.where(np.sum(np.abs(w), axis=(1, 3), keepdims=True) > 28.0, 0.5, 1.0)
    w = w.reshape(N, 8, 16, 4, 8, 16, 4)
    for i in still:
        w[:, :, i] = 0
        w[:, :, :, :, :, i] = 0
    return w
def drawn(rng, x, u, v, n, w):
    c, s = packed(np.ascontiguousarray(w).reshape(N, 128, 2048).astype(np.float32).astype(BF), rng)
    e = [np.stack([gtable(n[r, :, k]) for r in range(N)]) for k in range(3)]
    return {"x": x.reshape(N, 128, 4 * C).astype(np.float32).astype(BF), "u": u.reshape(N, 128, 512).astype(np.float32).astype(BF), "v": v.reshape(N, 128, 512).astype(np.float32).astype(BF), "n0": e[0], "n1": e[1], "n2": e[2], "wc": c, "ws": s}
def whole(x, u, s, i, k):
    for m in range(3):
        x[:, i + m] = ((s[:, :, None] >> (4 * m + np.arange(4))) & 1) * (2.0 ** (4 * m + np.arange(4)) * k)
        for h in range(0, 128, 16): u[h + i + m, h] = 1.0
def setup_inputs(rng):
    x, u, v = numbers_of(rng)
    return drawn(rng, x, u, v, graphs(rng), layers(rng))
def setup_inputs_ties(rng):
    x, u, v = numbers_of(rng)
    n, o = graphs(rng), rng.permutation(N)
    u[:, :, ::16] = 0
    for r in range(N):
        whole(x[r], u[r], rng.integers(0, 3, (8, C)), 0, 1.0)
        if o[r] == 0: u[r][:, ::16] = 0
        if o[r] == 1: u[r][:, ::16] *= -1
        if o[r] == 2: n[r] = np.stack([fours(rng) for g in range(8)])
    return drawn(rng, x, u, v, n, layers(rng, (0, 1, 2)))
def setup_inputs_near(rng):
    x, u, v = numbers_of(rng)
    o = rng.permutation(N) % 4
    x[:, :, 0] = 0
    x[:, :, 8:] = 0
    u[:, :, ::16] = 0
    for r in range(N):
        b, k = rng.integers(0, 2, (8, C)), rng.permutation(8)
        x[r, :, 0, :, 0] = [1.0, -1.0, 1.0, 0.0][o[r]]
        if o[r] < 3:
            whole(x[r], u[r], rng.integers(0, 256, (8, C)), 8, 2.0 ** -23)
            x[r, :, 11, :, 0] = 2.0 ** -10
        else:
            x[r, :, 12, :, 0] = 2.0 ** -28 * (1 - b)
            x[r, :, 13, :, 0] = 1.125 * 2.0 ** -28 * b
            for g in k[2:6]: x[r, g, 14, :, 0] = 2.0 ** -28
        for g in k[:4]: x[r, g, 0, rng.integers(C), 0] = rng.choice([-1.0, 1.0]) * 2.0 ** 26
        for h in range(0, 128, 16):
            u[r, h, h, 0] = 1.0
            u[r, h + 11, h, 0] = 1.0
            u[r, h + 12, h, 0] = 1.25
            u[r, h + 13, h, 0] = 1.125
            u[r, h + 14, h, 0] = -1.25
        if o[r] >= 2: u[r][:, ::16] *= 2.0 ** -30
    return drawn(rng, x, u, v, graphs(rng), layers(rng, (0, 8, 9, 10, 11, 12, 13, 14, 15)))
def setup_inputs_long(rng):
    x, u, v = numbers_of(rng)
    k = (N, 8, 8, C, 4)
    x[:, :, 8:] = rng.choice([-1.0, 1.0], k) * (1.0078125 + 0.015625 * rng.integers(0, 64, k)) * 2.0 ** -rng.integers(8, 15, k)
    x[:, :, 8, :, 0] = 1.96875
    u[:, :, ::16] = 0
    n, o, t = np.zeros((N, 8, 3, C), np.int64), (np.arange(N) + rng.integers(N)) % N // (N // 2), np.arange(C)
    for r in range(N):
        s = np.zeros((8, C), np.int64)
        for g in range(8):
            n[r, g], a = ring(rng, crossed(rng) if o[r] else opposite())
            s[g, a] = 512 * (1 - t % 2) + rng.permutation(C) if o[r] else C - 1 - t
        whole(x[r], u[r], s, 0, 1.0)
    return drawn(rng, x, u, v, n, layers(rng, (0, 1, 2)))
def setup_inputs_ends(rng):
    x, u, v = numbers_of(rng)
    o, k, h = rng.permutation(N) % 4, rng.permutation(N) % 2, rng.permutation(8)
    sg = rng.choice([-1.0, 1.0], (8, 16, 4))
    sg[h[:4]] = rng.choice([-1.0, 1.0])
    row, i = sg.reshape(128, 4), np.arange(128)
    n, w = graphs(rng), np.zeros((N, 128, 4, 128, 4), np.float32)
    for r in range(N):
        c = rng.permutation(C) % 2 == 0
        size, turn = 2.0 ** 30, np.ones((8, 16, 1, 1))
        if o[r] == 0:
            m, s = ring(rng, crossed(rng))
            n[r] = m
            a = 0.9 + 0.1 * rng.random((8, 16, C, 4))
            a[:, :, s[::2]] -= 0.15
            a *= 2.0 ** 26
        elif o[r] == 1:
            n[r] = np.stack([fours(rng) for g in range(8)])
            a = np.ones((8, 16, C, 4)) * np.where(c, 2.0 ** 26, 2.0 ** 25)[:, None]
            a[h[4:]] = np.where(c, 2.0 ** 25, 2.0 ** 26)[:, None]
            turn[h[4:]] = -1
        elif o[r] == 2: a, size = 2.0 ** -30, 2.0 ** -30
        else: a = np.where(c, 2.0 ** 26, 2.0 ** -30)[:, None]
        x[r] = a * sg[:, :, None]
        u[r] = size * row[:, None] * (turn * np.ones((1, 16, 1, 1))).reshape(128, 1, 1) * rng.choice([-1.0, 1.0], (1, 128, 1))
        v[r] = (size * row[:, None] * rng.choice([-1.0, 1.0], (1, 128, 1))).reshape(128, 512)
        if k[r]:
            for b in range(4): w[r, i, b, i, b] = 32
        else: w[r] = 0.0625 * row[:, None, None] * row.T[None, :, :, None]
    return drawn(rng, x, u, v, n, w)
def setup_inputs_spread(rng):
    x, u, v = numbers_of(rng)
    return drawn(rng, big(wide(rng, N, 128, 4 * C, cols=6)), u, v, graphs(rng), layers(rng))
def check_inputs(d):
    b = []
    for k, t in (("x", 26), ("u", 30), ("v", 30)):
        a = np.abs(d[k].astype(np.float32))
        if not (np.isfinite(a).all() and ((a == 0) | (a >= 2.0 ** -30) & (a <= 2.0 ** t)).all()): b.append("a value of " + k)
    none, least, most = [emit(mx_ref.quantize(np.full((128, 16), k, np.float32).astype(BF)))[1][0, 0] for k in (0.0, 2.0 ** -30, 2.0 ** 30)]
    i = np.arange(C)
    for r in range(N):
        n = [gentries(d[k][r]) for k in ("n0", "n1", "n2")]
        if not all([((e >= 0) & (e < C)).all() for e in n]): b.append("an entry of n0, n1 or n2")
        else:
            if any([(np.take_along_axis(e, e, axis=1) != i).any() or (e == i).any() for e in n]): b.append("n0, n1, n2: nodes not in pairs")
            if ((n[0] == n[1]) | (n[0] == n[2]) | (n[1] == n[2])).any(): b.append("n0, n1, n2: equal neighbours")
        if ((d["wc"][r] & 0x7F) == 0x7F).any(): b.append("wc: a code that is no number")
        s = mx_ref.live(d["ws"][r])
        if ((s != none) & ((s < least) | (s > most))).any(): b.append("ws: a scale out of range")
        if not (np.sum(np.abs(decode(pk(d["wc"][r], d["ws"][r]))).reshape(128, 512, 4), axis=(0, 2), dtype=np.float64) <= 32).all(): b.append("W: the sizes of a column")
    return b
def look(t, e):
    return np.where(e < 0, -1, np.take_along_axis(t, np.maximum(e, 0), axis=2))
def around(t, nb):
    return np.stack([np.take_along_axis(t, e, axis=2) for e in nb])
def best(t, nb):
    a = around(t, nb)
    return np.where(np.max(a, axis=0) < 0, -1, np.take_along_axis(nb, np.argmax(a, axis=0)[None], axis=0)[0])
def reference(x, u, v, n0, n1, n2, wc, ws):
    qu = [mx_ref.quantize(u[r]) for r in range(N)]
    lay = [pk(wc[r], ws[r]) for r in range(N)]
    now = [x[r] for r in range(N)]
    nb = np.stack([np.stack([gentries(n[r]) for r in range(N)]) for n in (n0, n1, n2)]).astype(np.int64)
    node = np.arange(C)
    for t in range(R):
        qx = [mx_ref.quantize(now[r]) for r in range(N)]
        full = [decode(qx[r]).astype(BF) for r in range(N)]
        score = np.stack([mx_ref.matmul(qu[r], qx[r])[::16] for r in range(N)]) + np.float32(0.0)
        z = C - 1 - np.argsort(np.argsort(-score, axis=2, kind="stable"), axis=2)
        state = np.zeros((N, 8, C), np.int64)
        for i in range(SWEEPS):
            key = np.where(state == 0, 512 * np.count_nonzero(around(state, nb) == 2, axis=0) + z, -1)
            win = key > np.max(around(key, nb), axis=0)
            state[win] = 1
            state[(state == 0) & np.any(around(win, nb), axis=0)] = 2
        coarse = state == 1
        o = np.argsort(~coarse, axis=2, kind="stable")
        slot, head = np.argsort(o, axis=2), o[:, :, :S]
        c = np.where(np.take_along_axis(coarse, head, axis=2), head, -1)
        fine = best(np.where(coarse, -1, z), nb)
        p1 = np.where(coarse, node, best(np.where(coarse, z, -1), nb))
        p2 = np.where(coarse, node, np.where(fine < 0, p1, look(p1, fine)))
        cf, s1, s2 = look(fine, c), look(slot, p1), look(slot, p2)
        qe = []
        for r in range(N):
            e = (gcols(full[r], c[r]).astype(np.float32) + gcols(full[r], cf[r]).astype(np.float32)) * np.float32(0.5)
            qe.append(mx_ref.quantize(e.astype(BF)))
        for r in range(N):
            h = tile([mx_ref.matmul(pick(lay[r], np.arange(128 * b, 128 * b + 128)), qe[r - 1]) * np.float32(0.03125) for b in range(4)])
            add = ((gcols(h, s1[r]).astype(np.float32) + gcols(h, s2[r]).astype(np.float32)) * np.float32(0.5)).astype(BF)
            now[r] = (full[r].astype(np.float32) + add.astype(np.float32)).astype(BF)
    y, op = np.zeros((N, 128, C), np.float32), np.zeros((N, 8, C), np.float32)
    oc, osc = np.zeros((N, 128, 4 * C), np.uint8), np.zeros((N, 16, C), np.uint8)
    for r in range(N):
        q = mx_ref.quantize(now[r])
        y[r] = mx_ref.matmul(mx_ref.quantize(v[r]), q)
        op[r] = p1[r]
        oc[r], osc[r] = emit(q)
    return {"y": y, "op": op, "oc": oc, "osc": osc}

@@ -1,0 +1,369 @@
+from concourse.mybir import dt, AluOpType as A, AxisListType, ActivationFunctionType as AF
+
+C, S, R, SWEEPS = 256, 128, 3, 8
+FS, HS = 272, 144
+U19 = 2.0 ** -19
+F32, B16, I32, U16, X4, U8 = "float32", "bfloat16", "int32", "uint16", "float8_e4m3fn_x4", "uint8"
+
+
+def _sb(n, d):
+    return ("sbuf", [128, n], d)
+
+
+SCRATCH = {
+    "xt": _sb(4 * C, B16), "ut": _sb(512, B16), "vt": _sb(512, B16), "ni": _sb(48, I32),
+    "qx": _sb(C, X4), "sx": _sb(C, U8), "qu": _sb(128, X4), "su": _sb(128, U8), "qv": _sb(128, X4), "sv": _sb(128, U8),
+    "qp": _sb(384, X4), "sp": _sb(384, U8), "qw": _sb(512, X4), "sw": _sb(512, U8),
+    "ot": _sb(512, B16), "qo": _sb(128, X4), "so": _sb(128, U8),
+    "idt": _sb(2048, B16), "qi": _sb(512, X4), "si": _sb(512, U8),
+    "cmp": _sb(4096, B16), "qc": _sb(1024, X4), "sc": _sb(1024, U8),
+    "iot": _sb(264, F32), "i19": _sb(C, F32), "i8": _sb(C, F32), "jm": _sb(512, B16),
+    "ne": _sb(512, B16), "d0": _sb(512, B16), "pi": _sb(2, I32), "pj": _sb(2, I32), "pm": _sb(2, F32), "ofc": _sb(2, F32),
+    "kh": _sb(8, B16), "cor": _sb(8, F32), "uli": _sb(24, I32), "ulo": _sb(24, U16),
+    "off": _sb(112, U16), "wn": _sb(768, F32), "wl": _sb(1024, F32), "sel": _sb(1024, F32),
+    "pv": _sb(C, F32), "ny": _sb(C, F32), "ny0": _sb(C, F32), "we": _sb(C, B16), "kk": _sb(C, F32), "k2": _sb(C, F32),
+    "tt": _sb(C, F32), "w0": _sb(C, B16), "w2": _sb(C, B16), "ff": _sb(C, B16), "pn": _sb(C, B16), "cc": _sb(C, F32),
+    "ww": _sb(C, B16), "pp": _sb(C, B16), "g2": _sb(C, F32), "u2": _sb(C, F32), "g3": _sb(4 * C, B16), "own": _sb(16, F32),
+    "js": _sb(8 * C, B16), "cs": _sb(8, F32), "ct": _sb(8, F32), "ofe": _sb(16, U16),
+    "g0": _sb(C, F32), "mf": _sb(264, F32), "mc": _sb(S, F32), "na": _sb(32, I32), "nb": _sb(32, I32),
+    "ps": _sb(C, F32), "aa": _sb(C, F32), "uu": _sb(C, F32), "mq": _sb(512, F32), "oft": _sb(32, U16),
+    "fh": _sb(4 * FS, B16), "ab": _sb(512, B16), "et": _sb(512, B16), "hh": _sb(4 * HS, B16),
+    "g1": _sb(4 * C, B16), "tb": _sb(4 * C, B16), "cw": _sb(HS, F32), "pw": _sb(C, F32), "yt": _sb(C, F32),
+    "pa": ("psum", [128, 4096], F32),
+}
+for _r in range(R):
+    SCRATCH["qe%d" % _r] = _sb(S, X4)
+    SCRATCH["se%d" % _r] = _sb(S, U8)
+    SCRATCH["ql%d" % _r] = _sb(S, X4)
+    SCRATCH["sl%d" % _r] = _sb(S, U8)
+NCS, NDS = 60, 24
+SEMAPHORES = ["c%d" % i for i in range(NCS)] + ["d%d" % i for i in range(NDS)] + ["arr%d" % i for i in range(R)] + ["sent"]
+
+
+def emit(g, T, ops):
+    queue = {"V": g.vector, "S": g.scalar, "T": g.tensor, "G": g, "Y": g.sync}
+    wr, rd, know, done, waits = {}, {}, {q: 0 for q in queue}, [], []
+    for i, o in enumerate(ops):
+        q, dep = o["q"], set()
+        for k in o["r"]:
+            if k in wr:
+                dep.add(wr[k])
+            if k[0] == "B":
+                dep.update(j for j in rd.get(k, []) if ops[j]["q"] != q)
+        for k in o["w"]:
+            if k in wr and not (o["acc"] and ops[wr[k]]["q"] == q):
+                dep.add(wr[k])
+            dep.update(rd.get(k, []))
+        need = []
+        for j in sorted(dep, reverse=True):
+            if not know[q] >> j & 1:
+                need.append(j)
+                know[q] |= done[j]
+        waits.append(need)
+        o["known"] = know[q]
+        done.append(know[q] | 1 << i)
+        for k in o["r"]:
+            rd.setdefault(k, []).append(i)
+        for k in o["w"]:
+            wr[k] = i
+            rd[k] = []
+    signals = set(j for w in waits for j in w)
+    last, count, where, nd = [None] * NCS, [0] * NCS, {}, [0]
+    for i, o in enumerate(ops):
+        eng = queue[o["q"]]
+        for j in waits[i]:
+            eng.wait_ge(T.sem[where[j][0]], where[j][1])
+        ins = o["f"]()
+        if i not in signals:
+            continue
+        if o["dma"]:
+            name = "d%d" % nd[0]
+            nd[0] += 1
+            for x in ins:
+                x.then_inc(T.sem[name], 16)
+            where[i] = (name, 16 * len(ins))
+        else:
+            s = [k for k in range(NCS) if last[k] is None or o["known"] >> last[k] & 1][0]
+            last[s] = i
+            count[s] += 1
+            ins.then_inc(T.sem["c%d" % s], 1)
+            where[i] = ("c%d" % s, count[s])
+
+
+def rank_program(g, core, T, topo):
+    rank = T.rank_of(core)
+    if rank is None:
+        return
+    nxt = T.cores[(rank + 1) % len(T.cores)]
+    rid, pid = topo.addr(nxt)[:2]
+    mask, nout = topo.mask(core, nxt), len(topo.engines(core, nxt))
+    nin = len(topo.engines(T.cores[rank - 1], core))
+    V, SC, PE = g.vector, g.scalar, g.tensor
+    ops = []
+
+    def op(q, f, r, w, dma=False, acc=False):
+        ops.append({"q": q, "f": f, "r": r.split(), "w": w.split(), "dma": dma, "acc": acc})
+
+    def tt(out, a, b, o, r, w):
+        op("V", lambda: V.tensor_tensor(out, a, b, o), r, w)
+
+    def ts(out, a, s1, o0, r, w, s2=None, o1=None):
+        if o1 is None:
+            op("V", lambda: V.tensor_scalar(out, a, s1, None, o0), r, w)
+        else:
+            op("V", lambda: V.tensor_scalar(out, a, s1, s2, o0, o1), r, w)
+
+    def cp(out, a, r, w):
+        op("V", lambda: V.tensor_copy(out, a), r, w)
+
+    def ms(out, c, w):
+        op("V", lambda: V.memset(out, c), "", w)
+
+    def act(out, a, r, w, f=AF.Copy, **kw):
+        op("S", lambda: SC.activation(out, a, f, **kw), r, w)
+
+    def qz(q, s, a, r, w):
+        op("V", lambda: V.quantize_mx(q, s, a), r, w)
+
+    def bank(b, n, a=0):
+        return T.pa[:, 512 * b + a:512 * b + n]
+
+    def mm(b, n, lq, ls, rq, rs, r, start=True, stop=True):
+        op("T", lambda: PE.matmul_mx(bank(b, n), lq, ls, rq, rs, start, stop), r, "B%d" % b, acc=not start)
+
+    def dma(q, pairs, r, w):
+        e = {"Y": g.sync, "S": SC}[q]
+        op(q, lambda: [e.dma_start(a, b) for a, b in pairs], r, w, dma=True)
+
+    def iota(out, pat, base, mul, w, flt=True):
+        if flt:
+            op("G", lambda: g.iota(out, pat, base, mul, allow_small_or_imprecise_dtypes=True), "", w)
+        else:
+            op("G", lambda: g.iota(out, pat, base, mul), "", w)
+
+    def scan(a, n, src, r, w):
+        op("V", lambda: V.tensor_tensor_scan(T.sel[:, a:a + n], T.d0[:, 0:n], src, 0.0, A.add, A.max), r + " d0", w)
+
+    def numbers(k, out, w):
+        ts(T.na[:, 0:k], T.sel[:, 15:16 * k:16], 1.0 / U19, A.mult, "sel sel1", "na")
+        ts(T.nb[:, 0:k], T.na[:, 0:k], 511, A.bitwise_and, "na", "nb")
+        cp(out, T.nb[:, 0:k], "nb", w)
+
+    N0, N1, N2, N10, N20, N01, N02 = range(7)
+    L0 = T.off[:, 0:16]
+
+    dma("S", [(T.ni[:, 0:16], T.n0[:]), (T.ni[:, 16:32], T.n1[:]), (T.ni[:, 32:48], T.n2[:])], "", "ni")
+    dma("Y", [(T.ut[:], T.u[:])], "", "ut")
+    dma("Y", [(T.xt[:], T.x[:])], "", "x0 x1 x2 x3")
+    dma("Y", [(T.qw[:].bitcast(dt.uint8), T.wc[:]), (T.sw[:], T.ws[:])], "", "qw")
+    dma("Y", [(T.vt[:], T.v[:])], "", "vt")
+    iota(T.pi[:, 0:1], [[0, 1]], 0, 1, "pi", False)
+    iota(T.iot[:], [[1, 264]], 0, 0, "iot")
+    iota(T.uli[:, 0:8], [[16, 8]], 0, 0, "ul0", False)
+    iota(T.uli[:, 8:24], [[16, 2], [32, 4], [0, 2]], 0, 0, "ul1", False)
+    iota(T.jm[:], [[0, 32], [1, 16]], 0, 0, "jm")
+    iota(T.idt[:], [[0, 2048]], 1, 0, "idt")
+    op("G", lambda: g.affine_select(T.idt[:], T.idt[:], [[-1, 4], [-8, 128], [1, 4]], A.is_equal, 0.0, 0, 8), "idt", "idt")
+    ms(T.ot[:], 0.0, " ".join("o%d" % k for k in range(16)))
+    for b in range(4):
+        for t in range(4):
+            a = 4 * (32 * b + 16 * (t // 2)) + t
+            ms(T.ot[32 * b:32 * b + 32, a:a + 61:4], 2.0 ** -10, "o%d" % (4 * b + t))
+    ms(T.fh[:, C:4 * FS:FS], 0.0, "fz")
+    ms(T.hh[:, 0:4 * HS:HS], 0.0, "hz")
+    ms(T.mf[:, C:C + 8], C * U19, "mz")
+    ts(T.pj[:, 0:1], T.pi[:, 0:1], 15, A.bitwise_and, "pi", "pj")
+    ms(T.cw[:, 0:1], -1.0, "cz")
+    cp(T.pm[:, 0:1], T.pj[:, 0:1], "pj", "pm")
+    qz(T.qo[:], T.so[:], T.ot[:], " ".join("o%d" % k for k in range(16)), "qo")
+    act(T.i8[:], T.iot[:, 0:C], "iot", "i8", scale=2.0 ** -8)
+    act(T.i19[:], T.iot[:, 0:C], "iot", "i19", scale=U19)
+    cp(T.ulo[:], T.uli[:], "ul0 ul1", "ulo")
+    cp(T.off[:, 0:48], T.ni[:], "ni", "l")
+    act(T.wn[:, C:3 * C], T.i8[:].indirect(T.off[:, 16:48]), "i8 l", "wn")
+    ts(T.ofc[:, 0:1], T.pm[:, 0:1], -2.0, A.mult, "pm", "ofc", 30.0, A.add)
+    ts(T.ne[:], T.jm[:], T.pm[:, 0:1], A.not_equal, "jm pm", "ne")
+    qz(T.qu[:], T.su[:], T.ut[:], "ut", "qu")
+    cp(T.qp[:].bitcast(dt.uint32), T.qu[:].bitcast(dt.uint32).indirect(T.ulo[:]), "qu ulo", "qp")
+    act(T.sp[:], T.su[:].indirect(T.ulo[:]), "qu ulo", "sp")
+    act(T.wl[:, 0:C], T.wn[:, C:2 * C].indirect(L0), "wn l", "wl0")
+    act(T.wl[:, C:2 * C], T.wn[:, 2 * C:3 * C].indirect(L0), "wn l", "wl00")
+
+    XK = "x0 x1 x2 x3"
+    for rd in range(R):
+        qe, se, ql, sl = [T[n + str(rd)] for n in ("qe", "se", "ql", "sl")]
+        qz(T.qx[:], T.sx[:], T.xt[:], XK, "qx")
+        for b, a in ((0, 0), (1, 128), (2, 256), (3, 128)):
+            mm(b, C, T.qp[:, a:a + 128], T.sp[:, a:a + 128], T.qx[:], T.sx[:], "qp sp qx")
+        if rd == 0:
+            ts(T.d0[:], T.ne[:], 66.0, A.mult, "ne", "d0", -64.0, A.add)
+        op("V", lambda: V.transpose(T.pv[:], bank(0, C)), "B0", "pv")
+
+        def slot(k, t):
+            return T.cmp[:, 1024 * k + t:1024 * (k + 1):4]
+
+        def cmp_v(c):
+            ts(slot(c // 2, c % 2), bank(1, C), T.pv[:, 32 * c:32 * c + 1], A.is_lt, "B1 pv", "m%d" % (c // 2 * 4 + c % 2))
+
+        def cmp_s(c, odd):
+            t = c % 2 + 2 * odd
+            act(slot(c // 2, t), bank(3 - odd, C), "pv B%d" % (3 - odd), "m%d" % (c // 2 * 4 + t), AF.Sign, scale=-1.0,
+                bias=T.pv[:, 32 * c + 16 * odd:32 * c + 16 * odd + 1])
+
+        def summed(k):
+            a = C * k
+            qz(T.qc[:, a:a + C], T.sc[:, a:a + C], T.cmp[:, 4 * a:4 * (a + C)], " ".join("m%d" % (4 * k + t) for t in range(4)), "qc%d" % k)
+            mm(0, C, T.qo[:], T.so[:], T.qc[:, a:a + C], T.sc[:, a:a + C], "qo qc%d" % k, k == 0, k == 3)
+
+        for c in range(8):
+            cmp_s(c, 1)
+        cmp_s(7, 0)
+        for c in range(4):
+            cmp_v(c)
+        summed(0)
+        cmp_v(4)
+        cmp_v(5)
+        summed(1)
+        cmp_v(6)
+        summed(2)
+        if rd == 0:
+            scan(0, 512, T.wl[:, 0:512], "wl0 wl00", "sel")
+            act(T.wn[:, 0:C], T.i8[:].indirect(L0), "i8 l", "wn0")
+        summed(3)
+        if rd == 0:
+            ts(T.off[:, 48:80], T.sel[:, 15:512:16], T.ofc[:, 0:1], A.subtract, "sel ofc", "ll", 256.0, A.mult)
+        for h in range(2):
+            tt(T.ny[:, S * h:S * h + S], bank(0, S * h + S, S * h), T.i19[:, S * h:S * h + S], A.add, "B0 i19", "ny_%d" % h)
+            act(T.k2[:, S * h:S * h + S], T.ny[:, S * h:S * h + S], "ny_%d" % h, "k2_%d" % h)
+        if rd == 0:
+            act(T.wl[:, 2 * C:4 * C], T.wn[:, 0:C].indirect(T.off[:, 16:48]), "wn0 l", "wl1")
+
+        def aside(s):
+            if s == 0:
+                act(T.ny0[:], T.ny[:].indirect(L0), "ny_0 ny_1 l", "ny0_0 ny0_1")
+            if s == 3:
+                if rd == 0:
+                    qz(T.qi[:], T.si[:], T.idt[:], "idt", "qi")
+                    ts(T.kh[:], T.iot[:, 0:128:16], T.pm[:, 0:1], A.add, "iot pm", "kh", 0.5, A.add)
+                    ts(T.cor[:], T.iot[:, 0:128:16], 256.0, A.add, "iot", "cor")
+                    ts(T.ofc[:, 1:2], T.pm[:, 0:1], U19 - 2.0, A.mult, "pm", "ofd", 30.5, A.add)
+                    ts(T.own[:], T.iot[:, 0:C:16], U19, A.mult, "iot ofd", "own", T.ofc[:, 1:2], A.add)
+                for b in range(4):
+                    mm(4 + b, C, T.qi[:, 128 * b:128 * b + 128], T.si[:, 128 * b:128 * b + 128], T.qx[:], T.sx[:], "qi qx")
+            if s in (4, 5):
+                for b in (2 * s - 8, 2 * s - 7):
+                    act(T.fh[:, FS * b:FS * b + C], bank(4 + b, C), "B%d" % (4 + b), "fh%d" % b, scale=0.5)
+
+        def step(out, win, k, plain, o, twin=None):
+            for h in range(2):
+                a = T[win][:, S * h:S * h + S] if k is None else T[win][:].indirect(T.off[:, 16 * k + 8 * h:16 * k + 8 * h + 8])
+                tt(T[out][:, S * h:S * h + S], a, T[plain][:, S * h:S * h + S], o, "l %s %s_0 %s_1 %s_%d" % ("lm" if k in (N01, N02) else "ll", win, win, plain, h), "%s_%d" % (out, h))
+                if twin:
+                    act(T[twin][:, S * h:S * h + S], T[out][:, S * h:S * h + S], "%s_%d" % (out, h), "%s_%d" % (twin, h))
+
+        for s in range(SWEEPS):
+            key = "kk" if s else "ny"
+            end = s == SWEEPS - 1
+            step("tt", key, N01 if end else N10, "k2", A.min)
+            step("tt", key, N02 if end else N20, "tt", A.min)
+            if end:
+                step("ww", key, N0, "tt", A.is_lt)
+                break
+            if rd == 0 and s == 0:
+                scan(512, 512, T.wl[:, 512:1024], "wl1", "sel1")
+            step("w0", key, N0, "tt", A.is_lt, "w2")
+            if rd == 0 and s == 0:
+                ts(T.off[:, 80:112], T.sel[:, 527:1024:16], T.ofc[:, 0:1], A.subtract, "sel1 ofc", "lm", 256.0, A.mult)
+            act(T.we[:], T.w0[:].indirect(L0), "w0_0 w0_1 l", "we_0 we_1")
+            step("ff", "w0", N01, "w2", A.max)
+            aside(s)
+            step("ff", "w0", N02, "ff", A.max)
+            step("pn", "we", None, "ff", A.subtract)
+            if s < SWEEPS - 2:
+                step("cc", "pn", N0, "ny", A.add)
+                step("cc", "pn", N1, "cc", A.add)
+                step("kk", "pn", N2, "cc", A.add, "k2")
+            else:
+                step("cc", "pn", N10, "ny0", A.add)
+                step("cc", "pn", N20, "cc", A.add)
+                step("kk", "pn", None, "cc", A.add, "k2")
+        WW = "ww_0 ww_1 "
+        op("V", lambda: V.tensor_tensor_scan(T.pp[:], T.ww[:], T.ww[:], 0.0, A.add, A.max), WW, "pp")
+        for m in range(8):
+            act(T.js[:, C * m + 16 * m:C * m + C], T.pp[:, 16 * m:C], "pp kh", "cs%d" % m, AF.Sign, scale=-1.0, bias=T.kh[:, m:m + 1], accum_out=T.cs[:, m:m + 1])
+        tt(T.g0[:], T.ww[:].indirect(L0), T.ny0[:], A.add, WW + "l ny0_0 ny0_1", "g0")
+        cp(T.g2[:], T.g0[:], "g0", "g2")
+        for k, plain in ((N01, "g2"), (N02, "mf")):
+            tt(T.mf[:, 0:C], T.g0[:].indirect(T.off[:, 16 * k:16 * k + 16]), T[plain][:, 0:C], A.min, "g0 g2 lm mf_0", "mf_0 mf_1")
+        tt(T.mq[:, C:2 * C], T.mf[:, 0:C], T.ww[:], A.add, WW + "mf_0 mf_1", "mq1")
+        tt(T.ct[:], T.cs[:], T.cor[:], A.add, "cor " + " ".join("cs%d" % m for m in range(8)), "ct")
+        LC, LF = T.ofe[:, 0:8], T.ofe[:, 8:16]
+        ts(LC, T.ct[:], 0.5, A.mult, "ct", "lc")
+        for b in range(4):
+            act(T.ab[:, S * b:S * b + S], T.fh[:, FS * b:FS * b + C + 1].indirect(LC), "fz fh%d lc" % b, "ab%d" % b)
+        cp(T.mc[:], T.mf[:].indirect(LC), "mf_0 mf_1 mz lc", "mc")
+        scan(0, S, T.mc[:], "mc", "sel")
+        numbers(8, LF, "lf")
+        for b in range(4):
+            tt(T.et[:, b:4 * S:4], T.fh[:, FS * b:FS * b + C + 1].indirect(LF), T.ab[:, S * b:S * b + S], A.add, "fz fh%d lf ab%d" % (b, b), "e%d" % b)
+        qz(qe[:], se[:], T.et[:], "e0 e1 e2 e3", "qe%d" % rd)
+
+        def send(qe=qe, se=se, ql=ql, sl=sl, rd=rd):
+            g.remote_dma(ql[:].bitcast(dt.uint8), qe[:].bitcast(dt.uint8), T.sem["arr%d" % rd], T.sem.sent, pid, rid, mask)
+            g.remote_dma(sl[:], se[:], T.sem["arr%d" % rd], T.sem.sent, pid, rid, mask)
+
+        op("G", send, "qe%d" % rd, "")
+        act(T.ps[:], T.pp[:], "pp", "ps", AF.Identity, scale=U19, bias=-1.0)
+        if rd == R - 1:
+            act(T.cw[:, 1:S + 1], T.iot[:].indirect(LC), "iot lc", "cw")
+        for h in range(2):
+            tt(T.aa[:, S * h:S * h + S], bank(0, S * h + S, S * h), T.ps[:, S * h:S * h + S], A.add, "B0 ps", "aa_%d" % h)
+        step("uu", "ww", None, "aa", A.mult, "u2")
+        scan(C, C, T.mq[:, C:2 * C], "mq1", "sel1")
+        step("mq", "uu", N0, "u2", A.min)
+        step("mq", "uu", N1, "mq", A.min)
+        tt(T.sel[:, C + 15:2 * C:16], T.sel[:, C + 15:2 * C:16], T.own[:], A.min, "sel1 own", "sel1")
+        step("mq", "uu", N2, "mq", A.min)
+        scan(0, C, T.mq[:, 0:C], "mq_0 mq_1", "sel")
+        numbers(32, T.oft[:], "lt")
+        if rd == 0:
+            qz(T.qv[:], T.sv[:], T.vt[:], "vt", "qv")
+        LS, LQ = T.oft[:, 0:16], T.oft[:, 16:32]
+        op("T", lambda rd=rd: PE.wait_ge(T.sem["arr%d" % rd], 2 * nin), "", "")
+        for b in range(4):
+            mm(b, S, T.qw[:, 128 * b:128 * b + 128], T.sw[:, 128 * b:128 * b + 128], ql[:], sl[:], "qw")
+        act(T.hh[:, 1:S + 1], bank(0, S), "B0", "hh0", scale=2.0 ** -6)
+        for b in range(1, 4):
+            ts(T.hh[:, HS * b + 1:HS * b + S + 1], bank(b, S), 2.0 ** -6, A.mult, "B%d" % b, "hh%d" % b)
+        for b in range(4):
+            act(T.g1[:, C * b:C * (b + 1)], T.hh[:, HS * b:HS * b + S + 1].indirect(LS), "hz hh%d lt" % b, "g1%d" % b)
+            if b in (1, 2):
+                act(T.g3[:, C * b:C * (b + 1)], T.g1[:, C * b:C * (b + 1)], "g1%d" % b, "g3%d" % b)
+        cp(T.g3[:, 0:C], T.g1[:, 0:C], "g10", "g30")
+        if rd == R - 1:
+            act(T.pw[:], T.cw[:, 0:S + 1].indirect(LS), "cz cw lt", "pw")
+            dma("Y", [(T.op[k:k + 1, :], T.pw[16 * k:16 * k + 1, :]) for k in range(8)], "pw", "out0")
+
+        def added(b):
+            tt(T.tb[:, C * b:C * (b + 1)], T.g1[:, C * b:C * (b + 1)].indirect(LQ), T.g3[:, C * b:C * (b + 1)], A.add, "g1%d g3%d lt" % (b, b), "tb%d" % b)
+
+        def state(b):
+            tt(T.xt[:, b:4 * C:4], T.tb[:, C * b:C * (b + 1)], bank(4 + b, C), A.add, "tb%d B%d" % (b, 4 + b), "x%d" % b)
+
+        added(0)
+        state(0)
+        added(1)
+        state(1)
+        added(2)
+        cp(T.g3[:, 3 * C:4 * C], T.g1[:, 3 * C:4 * C], "g13", "g33")
+        state(2)
+        added(3)
+        state(3)
+    qz(T.qx[:], T.sx[:], T.xt[:], XK, "qx")
+    mm(0, C, T.qv[:], T.sv[:], T.qx[:], T.sx[:], "qv qx")
+    dma("Y", [(T.oc[:], T.qx[:].bitcast(dt.uint8))], "qx", "out1")
+    dma("S", [(T.osc[4 * k:4 * k + 4, :], T.sx[32 * k:32 * k + 4, :]) for k in range(4)], "qx", "out2")
+    cp(T.yt[:], bank(0, C), "B0", "yt")
+    dma("Y", [(T.y[:], T.yt[:])], "yt", "out3")
+    op("G", lambda: g.wait_ge(T.sem.sent, 2 * R * nout), "out0 out1 out2 out3", "")
+    emit(g, T, ops)

@@ -1,6 +1,7 @@
 from concourse.mybir import dt, AluOpType as A, AxisListType, ActivationFunctionType as AF
 
 C, S, R, SWEEPS = 256, 128, 3, 8
+NV = 1
 FS, HS = 272, 144
 U19 = 2.0 ** -19
 F32, B16, I32, U16, X4, U8 = "float32", "bfloat16", "int32", "uint16", "float8_e4m3fn_x4", "uint8"
@@ -18,16 +19,18 @@ SCRATCH = {
     "idt": _sb(2048, B16), "qi": _sb(512, X4), "si": _sb(512, U8),
     "cmp": _sb(4096, B16), "qc": _sb(1024, X4), "sc": _sb(1024, U8),
     "iot": _sb(264, F32), "i19": _sb(C, F32), "i8": _sb(C, F32), "jm": _sb(512, B16),
-    "ne": _sb(512, B16), "d0": _sb(512, B16), "pi": _sb(2, I32), "pj": _sb(2, I32), "pm": _sb(2, F32), "ofc": _sb(2, F32),
+    "ne": _sb(512, B16), "d0": _sb(512, B16), "pi": _sb(2, I32), "pj": _sb(2, I32), "pm": _sb(2, F32), "ofc": _sb(4, F32),
     "kh": _sb(8, B16), "cor": _sb(8, F32), "uli": _sb(24, I32), "ulo": _sb(24, U16),
     "off": _sb(112, U16), "wn": _sb(768, F32), "wl": _sb(1024, F32), "sel": _sb(1024, F32),
     "pv": _sb(C, F32), "ny": _sb(C, F32), "ny0": _sb(C, F32), "we": _sb(C, B16), "kk": _sb(C, F32), "k2": _sb(C, F32),
     "tt": _sb(C, F32), "w0": _sb(C, B16), "w2": _sb(C, B16), "ff": _sb(C, B16), "pn": _sb(C, B16), "cc": _sb(C, F32),
+    "s1": _sb(C, F32), "s2": _sb(C, F32), "s3": _sb(C, B16), "s4": _sb(C, B16), "s5": _sb(C, B16), "yy": _sb(C, B16),
     "ww": _sb(C, B16), "pp": _sb(C, B16), "g2": _sb(C, F32), "u2": _sb(C, F32), "g3": _sb(4 * C, B16), "own": _sb(16, F32),
-    "js": _sb(8 * C, B16), "cs": _sb(8, F32), "ct": _sb(8, F32), "ofe": _sb(16, U16),
-    "g0": _sb(C, F32), "mf": _sb(264, F32), "mc": _sb(S, F32), "na": _sb(32, I32), "nb": _sb(32, I32),
-    "ps": _sb(C, F32), "aa": _sb(C, F32), "uu": _sb(C, F32), "mq": _sb(512, F32), "oft": _sb(32, U16),
-    "fh": _sb(4 * FS, B16), "ab": _sb(512, B16), "et": _sb(512, B16), "hh": _sb(4 * HS, B16),
+    "js": _sb(8 * C, B16), "cs": _sb(8, F32), "ct": _sb(8, F32), "ofe": _sb(24, U16),
+    "g0": _sb(C, F32), "mf": _sb(C, F32), "mc": _sb(C, F32), "na": _sb(32, I32), "nb": _sb(32, I32),
+    "ps": _sb(C, F32), "aa": _sb(C, F32), "uu": _sb(C, F32), "mq": _sb(C, F32), "oft": _sb(32, U16),
+    "ws2": _sb(C, B16), "ow1": _sb(16, F32), "ow2": _sb(16, F32),
+    "fh": _sb(4 * C, B16), "ab": _sb(4 * C, B16), "ew": _sb(4 * FS, B16), "et": _sb(512, B16), "hh": _sb(4 * HS, B16),
     "g1": _sb(4 * C, B16), "tb": _sb(4 * C, B16), "cw": _sb(HS, F32), "pw": _sb(C, F32), "yt": _sb(C, F32),
     "pa": ("psum", [128, 4096], F32),
 }
@@ -145,16 +148,16 @@ def rank_program(g, core, T, topo):
         op("V", lambda: V.tensor_tensor_scan(T.sel[:, a:a + n], T.d0[:, 0:n], src, 0.0, A.add, A.max), r + " d0", w)
 
     def numbers(k, out, w):
-        ts(T.na[:, 0:k], T.sel[:, 15:16 * k:16], 1.0 / U19, A.mult, "sel sel1", "na")
-        ts(T.nb[:, 0:k], T.na[:, 0:k], 511, A.bitwise_and, "na", "nb")
-        cp(out, T.nb[:, 0:k], "nb", w)
+        return [lambda: ts(T.na[:, 0:k], T.sel[:, 15:16 * k:16], 1.0 / U19, A.mult, "sel sel1", "na"),
+                lambda: ts(T.nb[:, 0:k], T.na[:, 0:k], 511, A.bitwise_and, "na", "nb"),
+                lambda: cp(out, T.nb[:, 0:k], "nb", w)]
 
     N0, N1, N2, N10, N20, N01, N02 = range(7)
     L0 = T.off[:, 0:16]
 
     dma("S", [(T.ni[:, 0:16], T.n0[:]), (T.ni[:, 16:32], T.n1[:]), (T.ni[:, 32:48], T.n2[:])], "", "ni")
     dma("Y", [(T.ut[:], T.u[:])], "", "ut")
-    dma("Y", [(T.xt[:], T.x[:])], "", "x0 x1 x2 x3")
+    dma("Y", [(T.xt[:], T.x[:])], "", "x0 x1 x2 x3 x4")
     dma("Y", [(T.qw[:].bitcast(dt.uint8), T.wc[:]), (T.sw[:], T.ws[:])], "", "qw")
     dma("Y", [(T.vt[:], T.v[:])], "", "vt")
     iota(T.pi[:, 0:1], [[0, 1]], 0, 1, "pi", False)
@@ -169,9 +172,8 @@ def rank_program(g, core, T, topo):
         for t in range(4):
             a = 4 * (32 * b + 16 * (t // 2)) + t
             ms(T.ot[32 * b:32 * b + 32, a:a + 61:4], 2.0 ** -10, "o%d" % (4 * b + t))
-    ms(T.fh[:, C:4 * FS:FS], 0.0, "fz")
+    ms(T.ew[:, C:4 * FS:FS], 0.0, "fz")
     ms(T.hh[:, 0:4 * HS:HS], 0.0, "hz")
-    ms(T.mf[:, C:C + 8], C * U19, "mz")
     ts(T.pj[:, 0:1], T.pi[:, 0:1], 15, A.bitwise_and, "pi", "pj")
     ms(T.cw[:, 0:1], -1.0, "cz")
     cp(T.pm[:, 0:1], T.pj[:, 0:1], "pj", "pm")
@@ -189,35 +191,53 @@ def rank_program(g, core, T, topo):
     act(T.wl[:, 0:C], T.wn[:, C:2 * C].indirect(L0), "wn l", "wl0")
     act(T.wl[:, C:2 * C], T.wn[:, 2 * C:3 * C].indirect(L0), "wn l", "wl00")
 
-    XK = "x0 x1 x2 x3"
+    def packed():
+        qz(T.qx[:, 0:S], T.sx[:, 0:S], T.xt[:, 0:4 * S], "x0 x1 x2 x3", "qx")
+        qz(T.qx[:, S:C], T.sx[:, S:C], T.xt[:, 4 * S:4 * C], "x0 x1 x2 x4", "qy")
+
+    def half(n, h):
+        return T[n][:, S * h:S * h + S]
+
+    def picked(win, k, hs):
+        return T[win][:].indirect(T.off[:, 16 * k + 8 * hs[0]:16 * k + 8 * hs[-1] + 8]), "l %s %s_0 %s_1" % ("lm" if k in (N01, N02) else "ll", win, win)
+
+    def step(out, win, k, plain, o, hs=(0, 1)):
+        for h in hs:
+            a, r = (half(win, h), "%s_%d" % (win, h)) if k is None else picked(win, k, [h])
+            tt(half(out, h), a, half(plain, h), o, "%s %s_%d" % (r, plain, h), "%s_%d" % (out, h))
+
+    def fetch(out, win, k, hs):
+        a, r = picked(win, k, hs)
+        act(T[out][:, S * hs[0]:S * hs[-1] + S], a, r, " ".join("%s_%d" % (out, h) for h in hs))
+
+    def twin(out, src, h):
+        act(half(out, h), half(src, h), "%s_%d" % (src, h), "%s_%d" % (out, h))
+
     for rd in range(R):
         qe, se, ql, sl = [T[n + str(rd)] for n in ("qe", "se", "ql", "sl")]
-        qz(T.qx[:], T.sx[:], T.xt[:], XK, "qx")
+        packed()
         for b, a in ((0, 0), (1, 128), (2, 256), (3, 128)):
-            mm(b, C, T.qp[:, a:a + 128], T.sp[:, a:a + 128], T.qx[:], T.sx[:], "qp sp qx")
+            mm(b, C, T.qp[:, a:a + 128], T.sp[:, a:a + 128], T.qx[:], T.sx[:], "qp sp qx qy")
         if rd == 0:
             ts(T.d0[:], T.ne[:], 66.0, A.mult, "ne", "d0", -64.0, A.add)
-        op("V", lambda: V.transpose(T.pv[:], bank(0, C)), "B0", "pv")
+        for h in range(2):
+            op("V", lambda h=h: V.transpose(half("pv", h), bank(0, S * h + S, S * h)), "B0", "pv%d" % h)
 
         def slot(k, t):
             return T.cmp[:, 1024 * k + t:1024 * (k + 1):4]
 
         def cmp_v(c):
-            ts(slot(c // 2, c % 2), bank(1, C), T.pv[:, 32 * c:32 * c + 1], A.is_lt, "B1 pv", "m%d" % (c // 2 * 4 + c % 2))
-
-        def cmp_s(c, odd):
-            t = c % 2 + 2 * odd
-            act(slot(c // 2, t), bank(3 - odd, C), "pv B%d" % (3 - odd), "m%d" % (c // 2 * 4 + t), AF.Sign, scale=-1.0,
-                bias=T.pv[:, 32 * c + 16 * odd:32 * c + 16 * odd + 1])
+            ts(slot(c // 2, c % 2), bank(1, C), T.pv[:, 32 * c:32 * c + 1], A.is_lt, "B1 pv%d" % (c // 4), "m%d" % (c // 2 * 4 + c % 2))
 
         def summed(k):
             a = C * k
-            qz(T.qc[:, a:a + C], T.sc[:, a:a + C], T.cmp[:, 4 * a:4 * (a + C)], " ".join("m%d" % (4 * k + t) for t in range(4)), "qc%d" % k)
+            qz(T.qc[:, a:a + C], T.sc[:, a:a + C], T.cmp[:, 4 * a:4 * (a + C)], " ".join("m%d" % (4 * k + t) for t in range(4 + (k == 3))), "qc%d" % k)
             mm(0, C, T.qo[:], T.so[:], T.qc[:, a:a + C], T.sc[:, a:a + C], "qo qc%d" % k, k == 0, k == 3)
 
         for c in range(8):
-            cmp_s(c, 1)
-        cmp_s(7, 0)
+            act(slot(c // 2, c % 2 + 2), bank(2, C), "pv%d B2" % (c // 4), "m%d" % (c // 2 * 4 + c % 2 + 2), AF.Sign, scale=-1.0,
+                bias=T.pv[:, 32 * c + 16:32 * c + 17])
+        act(slot(3, 1), bank(3, C), "pv1 B3", "m13 m16", AF.Sign, scale=-1.0, bias=T.pv[:, 224:225])
         for c in range(4):
             cmp_v(c)
         summed(0)
@@ -233,79 +253,119 @@ def rank_program(g, core, T, topo):
         if rd == 0:
             ts(T.off[:, 48:80], T.sel[:, 15:512:16], T.ofc[:, 0:1], A.subtract, "sel ofc", "ll", 256.0, A.mult)
         for h in range(2):
-            tt(T.ny[:, S * h:S * h + S], bank(0, S * h + S, S * h), T.i19[:, S * h:S * h + S], A.add, "B0 i19", "ny_%d" % h)
-            act(T.k2[:, S * h:S * h + S], T.ny[:, S * h:S * h + S], "ny_%d" % h, "k2_%d" % h)
+            tt(half("ny", h), bank(0, S * h + S, S * h), half("i19", h), A.add, "B0 i19", "ny_%d" % h)
+            twin("k2", "ny", h)
+        LF, LC = T.ofe[:, 0:16], T.ofe[:, 16:24]
+
+        def unpack():
+            if rd == 0:
+                qz(T.qi[:], T.si[:], T.idt[:], "idt", "qi")
+            for b in range(4):
+                mm(4 + b, C, T.qi[:, 128 * b:128 * b + 128], T.si[:, 128 * b:128 * b + 128], T.qx[:], T.sx[:], "qi qx qy")
+            scan(0, C, T.mc[:], "mc_0 mc_1", "sel")
+
+        def tables():
+            ts(T.kh[:], T.iot[:, 0:128:16], T.pm[:, 0:1], A.add, "iot pm", "kh", 0.5, A.add)
+            ts(T.cor[:, 0:NV], T.iot[:, 0:16 * NV:16], 2.0, A.mult, "iot", "co0")
+            ts(T.cor[:, NV:8], T.iot[:, 16 * NV:128:16], 256.0, A.add, "iot", "co1")
+            ts(T.ofc[:, 1:2], T.pm[:, 0:1], U19, A.mult, "pm", "ofd", 0.5, A.add)
+            ts(T.ofc[:, 2:3], T.pm[:, 0:1], -4.0, A.mult, "pm", "ofe", 60.0, A.add)
+
+        def mean(b, h):
+            a = C * b + S * h
+            tt(T.ew[:, FS * b + S * h:FS * b + S * h + S], T.fh[:, a:a + S], T.ab[:, a:a + S], A.add, "fh%d ab%d" % (b, b), "ew%d%d" % (b, h))
+
+        fill, side = {3: unpack}, {1: lambda: fetch("mc", "tt", N0, [0, 1]), 2: lambda: fetch("ny0", "ny", N0, [0, 1])}
+        for k, f in enumerate(numbers(16, LF, "lf")):
+            fill[4 + k] = f
         if rd == 0:
-            act(T.wl[:, 2 * C:4 * C], T.wn[:, 0:C].indirect(T.off[:, 16:48]), "wn0 l", "wl1")
+            fill[7] = tables
+            fill[8] = lambda: ts(T.own[:], T.iot[:, 0:C:16], U19, A.mult, "iot ofd", "own", T.ofc[:, 1:2], A.add)
+        for b in range(4):
+            side[5 + b] = lambda b=b: act(T.fh[:, C * b:C * b + C], bank(4 + b, C), "B%d" % (4 + b), "fh%d" % b, scale=0.5)
+            side[9 + b] = lambda b=b: act(T.ab[:, C * b:C * b + C], T.fh[:, C * b:C * b + C].indirect(LF), "fh%d lf" % b, "ab%d" % b)
+        for k in range(8):
+            fill[13 + k] = lambda k=k: mean(k // 2, k % 2)
 
-        def aside(s):
-            if s == 0:
-                act(T.ny0[:], T.ny[:].indirect(L0), "ny_0 ny_1 l", "ny0_0 ny0_1")
-            if s == 3:
-                if rd == 0:
-                    qz(T.qi[:], T.si[:], T.idt[:], "idt", "qi")
-                    ts(T.kh[:], T.iot[:, 0:128:16], T.pm[:, 0:1], A.add, "iot pm", "kh", 0.5, A.add)
-                    ts(T.cor[:], T.iot[:, 0:128:16], 256.0, A.add, "iot", "cor")
-                    ts(T.ofc[:, 1:2], T.pm[:, 0:1], U19 - 2.0, A.mult, "pm", "ofd", 30.5, A.add)
-                    ts(T.own[:], T.iot[:, 0:C:16], U19, A.mult, "iot ofd", "own", T.ofc[:, 1:2], A.add)
-                for b in range(4):
-                    mm(4 + b, C, T.qi[:, 128 * b:128 * b + 128], T.si[:, 128 * b:128 * b + 128], T.qx[:], T.sx[:], "qi qx")
-            if s in (4, 5):
-                for b in (2 * s - 8, 2 * s - 7):
-                    act(T.fh[:, FS * b:FS * b + C], bank(4 + b, C), "B%d" % (4 + b), "fh%d" % b, scale=0.5)
-
-        def step(out, win, k, plain, o, twin=None):
-            for h in range(2):
-                a = T[win][:, S * h:S * h + S] if k is None else T[win][:].indirect(T.off[:, 16 * k + 8 * h:16 * k + 8 * h + 8])
-                tt(T[out][:, S * h:S * h + S], a, T[plain][:, S * h:S * h + S], o, "l %s %s_0 %s_1 %s_%d" % ("lm" if k in (N01, N02) else "ll", win, win, plain, h), "%s_%d" % (out, h))
-                if twin:
-                    act(T[twin][:, S * h:S * h + S], T[out][:, S * h:S * h + S], "%s_%d" % (out, h), "%s_%d" % (twin, h))
+        def room(table, k):
+            if k in table:
+                table[k]()
 
         for s in range(SWEEPS):
             key = "kk" if s else "ny"
             end = s == SWEEPS - 1
-            step("tt", key, N01 if end else N10, "k2", A.min)
-            step("tt", key, N02 if end else N20, "tt", A.min)
+            la, lb = (N01, N02) if end else (N10, N20)
+            fetch("s1", key, lb, [1])
+            fetch("s2", key, N0, [0, 1])
+            if rd == 0 and s == 0:
+                act(T.wl[:, 2 * C:4 * C], T.wn[:, 0:C].indirect(T.off[:, 16:48]), "wn0 l", "wl1")
+            room(side, 3 * s)
+            step("tt", key, la, "k2", A.min)
+            step("tt", key, lb, "tt", A.min, [0])
+            step("tt", "s1", None, "tt", A.min, [1])
             if end:
-                step("ww", key, N0, "tt", A.is_lt)
+                step("ww", "s2", None, "tt", A.is_lt)
                 break
+            step("w0", "s2", None, "tt", A.is_lt)
+            cp(half("w2", 0), half("w0", 0), "w0_0", "w2_0")
+            twin("w2", "w0", 1)
             if rd == 0 and s == 0:
                 scan(512, 512, T.wl[:, 512:1024], "wl1", "sel1")
-            step("w0", key, N0, "tt", A.is_lt, "w2")
-            if rd == 0 and s == 0:
                 ts(T.off[:, 80:112], T.sel[:, 527:1024:16], T.ofc[:, 0:1], A.subtract, "sel1 ofc", "lm", 256.0, A.mult)
-            act(T.we[:], T.w0[:].indirect(L0), "w0_0 w0_1 l", "we_0 we_1")
+            fetch("s3", "w0", N02, [1])
+            fetch("we", "w0", N0, [0, 1])
+            room(side, 3 * s + 1)
+            room(fill, 3 * s)
             step("ff", "w0", N01, "w2", A.max)
-            aside(s)
-            step("ff", "w0", N02, "ff", A.max)
+            step("ff", "w0", N02, "ff", A.max, [0])
+            step("ff", "s3", None, "ff", A.max, [1])
             step("pn", "we", None, "ff", A.subtract)
+            room(fill, 3 * s + 1)
             if s < SWEEPS - 2:
+                fetch("s4", "pn", N1, [1])
+                fetch("s5", "pn", N2, [1])
+                fetch("s5", "pn", N2, [0])
+                room(side, 3 * s + 2)
                 step("cc", "pn", N0, "ny", A.add)
-                step("cc", "pn", N1, "cc", A.add)
-                step("kk", "pn", N2, "cc", A.add, "k2")
+                step("cc", "pn", N1, "cc", A.add, [0])
+                step("yy", "s4", None, "s5", A.add, [1])
+                step("kk", "s5", None, "cc", A.add, [0])
+                twin("k2", "kk", 0)
+                step("kk", "yy", None, "cc", A.add, [1])
             else:
+                fetch("s4", "pn", N20, [0, 1])
                 step("cc", "pn", N10, "ny0", A.add)
-                step("cc", "pn", N20, "cc", A.add)
-                step("kk", "pn", None, "cc", A.add, "k2")
+                step("yy", "s4", None, "pn", A.add)
+                step("kk", "yy", None, "cc", A.add, [0])
+                twin("k2", "kk", 0)
+                step("kk", "yy", None, "cc", A.add, [1])
+            twin("k2", "kk", 1)
+            room(fill, 3 * s + 2)
         WW = "ww_0 ww_1 "
         op("V", lambda: V.tensor_tensor_scan(T.pp[:], T.ww[:], T.ww[:], 0.0, A.add, A.max), WW, "pp")
-        for m in range(8):
-            act(T.js[:, C * m + 16 * m:C * m + C], T.pp[:, 16 * m:C], "pp kh", "cs%d" % m, AF.Sign, scale=-1.0, bias=T.kh[:, m:m + 1], accum_out=T.cs[:, m:m + 1])
         tt(T.g0[:], T.ww[:].indirect(L0), T.ny0[:], A.add, WW + "l ny0_0 ny0_1", "g0")
+        for m in range(8):
+            a, j = T.pp[:, 16 * m:C], T.js[:, C * m + 16 * m:C * m + C]
+            if m < NV:
+                ts(j, a, T.kh[:, m:m + 1], A.is_lt, "pp kh", "js%d" % m, 2.0, A.mult)
+            else:
+                act(j, a, "pp kh", "cs%d" % m, AF.Sign, scale=-1.0, bias=T.kh[:, m:m + 1], accum_out=T.cs[:, m:m + 1])
         cp(T.g2[:], T.g0[:], "g0", "g2")
-        for k, plain in ((N01, "g2"), (N02, "mf")):
-            tt(T.mf[:, 0:C], T.g0[:].indirect(T.off[:, 16 * k:16 * k + 16]), T[plain][:, 0:C], A.min, "g0 g2 lm mf_0", "mf_0 mf_1")
-        tt(T.mq[:, C:2 * C], T.mf[:, 0:C], T.ww[:], A.add, WW + "mf_0 mf_1", "mq1")
-        tt(T.ct[:], T.cs[:], T.cor[:], A.add, "cor " + " ".join("cs%d" % m for m in range(8)), "ct")
-        LC, LF = T.ofe[:, 0:8], T.ofe[:, 8:16]
+        for m in range(NV):
+            op("V", lambda m=m: V.tensor_reduce(T.cs[:, m:m + 1], T.js[:, C * m + 16 * m:C * m + C], AxisListType.X, A.add), "js%d" % m, "cs%d" % m)
+
+        def least(out, win, k, plain, r, w):
+            tt(out, win.indirect(T.off[:, 16 * k:16 * k + 16]), plain, A.min, r + " l lm", w)
+
+        least(T.mf[:], T.g0[:], N01, T.g2[:], "g0 g2", "mf")
+        act(T.ps[:], T.pp[:], "pp", "ps", AF.Identity, scale=U19, bias=-1.0)
+        tt(T.ct[:], T.cs[:], T.cor[:], A.add, "co0 co1 " + " ".join("cs%d" % m for m in range(8)), "ct")
+        op("V", lambda: V.tensor_tensor_scan(T.ws2[:], T.d0[:, 0:C], T.ww[:], 0.0, A.add, A.max), WW + "d0", "ws2")
         ts(LC, T.ct[:], 0.5, A.mult, "ct", "lc")
+        tt(T.aa[:], bank(0, C), T.ps[:], A.add, "B0 ps", "aa")
         for b in range(4):
-            act(T.ab[:, S * b:S * b + S], T.fh[:, FS * b:FS * b + C + 1].indirect(LC), "fz fh%d lc" % b, "ab%d" % b)
-        cp(T.mc[:], T.mf[:].indirect(LC), "mf_0 mf_1 mz lc", "mc")
-        scan(0, S, T.mc[:], "mc", "sel")
-        numbers(8, LF, "lf")
-        for b in range(4):
-            tt(T.et[:, b:4 * S:4], T.fh[:, FS * b:FS * b + C + 1].indirect(LF), T.ab[:, S * b:S * b + S], A.add, "fz fh%d lf ab%d" % (b, b), "e%d" % b)
+            (cp if b < 2 else act)(T.et[:, b:4 * S:4], T.ew[:, FS * b:FS * b + C + 1].indirect(LC), "fz ew%d0 ew%d1 lc" % (b, b), "e%d" % b)
+        tt(T.uu[:, 0:S], T.ww[:, 0:S], T.aa[:, 0:S], A.mult, WW + "aa", "uu")
         qz(qe[:], se[:], T.et[:], "e0 e1 e2 e3", "qe%d" % rd)
 
         def send(qe=qe, se=se, ql=ql, sl=sl, rd=rd):
@@ -313,33 +373,34 @@ def rank_program(g, core, T, topo):
             g.remote_dma(sl[:], se[:], T.sem["arr%d" % rd], T.sem.sent, pid, rid, mask)
 
         op("G", send, "qe%d" % rd, "")
-        act(T.ps[:], T.pp[:], "pp", "ps", AF.Identity, scale=U19, bias=-1.0)
+        tt(T.uu[:, S:C], T.ww[:, S:C], T.aa[:, S:C], A.mult, WW + "aa", "uv")
+        act(T.u2[:], T.uu[:], "uu uv", "u2")
         if rd == R - 1:
             act(T.cw[:, 1:S + 1], T.iot[:].indirect(LC), "iot lc", "cw")
-        for h in range(2):
-            tt(T.aa[:, S * h:S * h + S], bank(0, S * h + S, S * h), T.ps[:, S * h:S * h + S], A.add, "B0 ps", "aa_%d" % h)
-        step("uu", "ww", None, "aa", A.mult, "u2")
-        scan(C, C, T.mq[:, C:2 * C], "mq1", "sel1")
-        step("mq", "uu", N0, "u2", A.min)
-        step("mq", "uu", N1, "mq", A.min)
-        tt(T.sel[:, C + 15:2 * C:16], T.sel[:, C + 15:2 * C:16], T.own[:], A.min, "sel1 own", "sel1")
-        step("mq", "uu", N2, "mq", A.min)
-        scan(0, C, T.mq[:, 0:C], "mq_0 mq_1", "sel")
-        numbers(32, T.oft[:], "lt")
+        ts(T.ow1[:], T.ws2[:, 15:C:16], -1.0, A.mult, "ws2 ofe", "ow1", T.ofc[:, 2:3], A.add)
+        least(T.mf[:], T.g0[:], N02, T.mf[:], "g0 mf", "mf")
+        tt(T.ow2[:], T.ow1[:], T.own[:], A.add, "own ow1", "ow2")
+        least(T.mq[:], T.uu[:], N0, T.u2[:], "uu uv u2", "ms")
+        scan(C, C, T.mf[:], "mf", "sel1")
+        least(T.mq[:], T.uu[:], N1, T.mq[:], "uu ms", "ms")
+        tt(T.sel[:, C + 15:2 * C:16], T.sel[:, C + 15:2 * C:16], T.ow2[:], A.min, "sel1 ow2", "sel1")
         if rd == 0:
             qz(T.qv[:], T.sv[:], T.vt[:], "vt", "qv")
+        least(T.mq[:], T.uu[:], N2, T.mq[:], "uu ms", "ms")
+        scan(0, C, T.mq[:], "ms", "sel")
+        for f in numbers(32, T.oft[:], "lt"):
+            f()
         LS, LQ = T.oft[:, 0:16], T.oft[:, 16:32]
         op("T", lambda rd=rd: PE.wait_ge(T.sem["arr%d" % rd], 2 * nin), "", "")
         for b in range(4):
             mm(b, S, T.qw[:, 128 * b:128 * b + 128], T.sw[:, 128 * b:128 * b + 128], ql[:], sl[:], "qw")
-        act(T.hh[:, 1:S + 1], bank(0, S), "B0", "hh0", scale=2.0 ** -6)
-        for b in range(1, 4):
-            ts(T.hh[:, HS * b + 1:HS * b + S + 1], bank(b, S), 2.0 ** -6, A.mult, "B%d" % b, "hh%d" % b)
-        for b in range(4):
-            act(T.g1[:, C * b:C * (b + 1)], T.hh[:, HS * b:HS * b + S + 1].indirect(LS), "hz hh%d lt" % b, "g1%d" % b)
-            if b in (1, 2):
-                act(T.g3[:, C * b:C * (b + 1)], T.g1[:, C * b:C * (b + 1)], "g1%d" % b, "g3%d" % b)
-        cp(T.g3[:, 0:C], T.g1[:, 0:C], "g10", "g30")
+        for b in range(5):
+            if b < 4:
+                act(T.hh[:, HS * b + 1:HS * b + S + 1], bank(b, S), "B%d" % b, "hh%d" % b, scale=2.0 ** -6)
+            if b:
+                act(T.g1[:, C * b - C:C * b], T.hh[:, HS * b - HS:HS * b - HS + S + 1].indirect(LS), "hz hh%d lt" % (b - 1), "g1%d" % (b - 1))
+        act(T.g3[:, 3 * C:4 * C], T.g1[:, 3 * C:4 * C], "g13", "g33")
+        cp(T.g3[:, 0:C], T.hh[:, 0:S + 1].indirect(LS), "hz hh0 lt", "g30")
         if rd == R - 1:
             act(T.pw[:], T.cw[:, 0:S + 1].indirect(LS), "cz cw lt", "pw")
             dma("Y", [(T.op[k:k + 1, :], T.pw[16 * k:16 * k + 1, :]) for k in range(8)], "pw", "out0")
@@ -347,22 +408,27 @@ def rank_program(g, core, T, topo):
         def added(b):
             tt(T.tb[:, C * b:C * (b + 1)], T.g1[:, C * b:C * (b + 1)].indirect(LQ), T.g3[:, C * b:C * (b + 1)], A.add, "g1%d g3%d lt" % (b, b), "tb%d" % b)
 
-        def state(b):
-            tt(T.xt[:, b:4 * C:4], T.tb[:, C * b:C * (b + 1)], bank(4 + b, C), A.add, "tb%d B%d" % (b, 4 + b), "x%d" % b)
+        def state(b, a=0, e=C):
+            tt(T.xt[:, 4 * a + b:4 * e:4], T.tb[:, C * b + a:C * b + e], bank(4 + b, e, a), A.add, "tb%d B%d" % (b, 4 + b), "x%d" % (b + (a > 0)))
+
+        def again(b):
+            cp(T.g3[:, C * b:C * (b + 1)], T.g1[:, C * b:C * (b + 1)], "g1%d" % b, "g3%d" % b)
 
         added(0)
+        again(1)
         state(0)
         added(1)
+        again(2)
         state(1)
         added(2)
-        cp(T.g3[:, 3 * C:4 * C], T.g1[:, 3 * C:4 * C], "g13", "g33")
-        state(2)
         added(3)
-        state(3)
-    qz(T.qx[:], T.sx[:], T.xt[:], XK, "qx")
-    mm(0, C, T.qv[:], T.sv[:], T.qx[:], T.sx[:], "qv qx")
-    dma("Y", [(T.oc[:], T.qx[:].bitcast(dt.uint8))], "qx", "out1")
-    dma("S", [(T.osc[4 * k:4 * k + 4, :], T.sx[32 * k:32 * k + 4, :]) for k in range(4)], "qx", "out2")
+        state(2)
+        state(3, 0, S)
+        state(3, S, C)
+    packed()
+    mm(0, C, T.qv[:], T.sv[:], T.qx[:], T.sx[:], "qv qx qy")
+    dma("Y", [(T.oc[:], T.qx[:].bitcast(dt.uint8))], "qx qy", "out1")
+    dma("S", [(T.osc[4 * k:4 * k + 4, :], T.sx[32 * k:32 * k + 4, :]) for k in range(4)], "qx qy", "out2")
     cp(T.yt[:], bank(0, C), "B0", "yt")
     dma("Y", [(T.y[:], T.yt[:])], "yt", "out3")
     op("G", lambda: g.wait_ge(T.sem.sent, 2 * R * nout), "out0 out1 out2 out3", "")

@@ -1,7 +1,7 @@
 from concourse.mybir import dt, AluOpType as A, AxisListType, ActivationFunctionType as AF
 
 C, S, R, SWEEPS = 256, 128, 3, 8
-NV = 1
+NV = 2
 FS, HS = 272, 144
 U19 = 2.0 ** -19
 F32, B16, I32, U16, X4, U8 = "float32", "bfloat16", "int32", "uint16", "float8_e4m3fn_x4", "uint8"
@@ -24,8 +24,8 @@ SCRATCH = {
     "off": _sb(112, U16), "wn": _sb(768, F32), "wl": _sb(1024, F32), "sel": _sb(1024, F32),
     "pv": _sb(C, F32), "ny": _sb(C, F32), "ny0": _sb(C, F32), "we": _sb(C, B16), "kk": _sb(C, F32), "k2": _sb(C, F32),
     "tt": _sb(C, F32), "w0": _sb(C, B16), "w2": _sb(C, B16), "ff": _sb(C, B16), "pn": _sb(C, B16), "cc": _sb(C, F32),
-    "s1": _sb(C, F32), "s2": _sb(C, F32), "s3": _sb(C, B16), "s4": _sb(C, B16), "s5": _sb(C, B16), "yy": _sb(C, B16),
-    "ww": _sb(C, B16), "pp": _sb(C, B16), "g2": _sb(C, F32), "u2": _sb(C, F32), "g3": _sb(4 * C, B16), "own": _sb(16, F32),
+    "s1": _sb(C, F32), "s2": _sb(C, F32), "s3": _sb(C, B16), "s4": _sb(C, B16), "yy": _sb(C, B16),
+    "ww": _sb(C, B16), "pp": _sb(C, B16), "g2": _sb(C, F32), "g3": _sb(4 * C, B16), "own": _sb(16, F32),
     "js": _sb(8 * C, B16), "cs": _sb(8, F32), "ct": _sb(8, F32), "ofe": _sb(24, U16),
     "g0": _sb(C, F32), "mf": _sb(C, F32), "mc": _sb(C, F32), "na": _sb(32, I32), "nb": _sb(32, I32),
     "ps": _sb(C, F32), "aa": _sb(C, F32), "uu": _sb(C, F32), "mq": _sb(C, F32), "oft": _sb(32, U16),
@@ -148,9 +148,10 @@ def rank_program(g, core, T, topo):
         op("V", lambda: V.tensor_tensor_scan(T.sel[:, a:a + n], T.d0[:, 0:n], src, 0.0, A.add, A.max), r + " d0", w)
 
     def numbers(k, out, w):
-        return [lambda: ts(T.na[:, 0:k], T.sel[:, 15:16 * k:16], 1.0 / U19, A.mult, "sel sel1", "na"),
-                lambda: ts(T.nb[:, 0:k], T.na[:, 0:k], 511, A.bitwise_and, "na", "nb"),
-                lambda: cp(out, T.nb[:, 0:k], "nb", w)]
+        na, nb = T.na[:, 16 * k:16 * k + 16], T.nb[:, 16 * k:16 * k + 16]
+        return [lambda: ts(na, T.sel[:, C * k + 15:C * k + C:16], 1.0 / U19, A.mult, ("sel", "sel1")[k], "na%d" % k),
+                lambda: ts(nb, na, 511, A.bitwise_and, "na%d" % k, "nb%d" % k),
+                lambda: cp(out, nb, "nb%d" % k, w)]
 
     N0, N1, N2, N10, N20, N01, N02 = range(7)
     L0 = T.off[:, 0:16]
@@ -216,12 +217,17 @@ def rank_program(g, core, T, topo):
     for rd in range(R):
         qe, se, ql, sl = [T[n + str(rd)] for n in ("qe", "se", "ql", "sl")]
         packed()
-        for b, a in ((0, 0), (1, 128), (2, 256), (3, 128)):
-            mm(b, C, T.qp[:, a:a + 128], T.sp[:, a:a + 128], T.qx[:], T.sx[:], "qp sp qx qy")
+        mm(0, S, T.qp[:, 0:128], T.sp[:, 0:128], T.qx[:, 0:S], T.sx[:, 0:S], "qp sp qx")
+        for b in (1, 2):
+            mm(b, C, T.qp[:, 128 * b:128 * b + 128], T.sp[:, 128 * b:128 * b + 128], T.qx[:], T.sx[:], "qp sp qx qy")
+        mm(3, S, T.qp[:, 0:128], T.sp[:, 0:128], T.qx[:, S:C], T.sx[:, S:C], "qp sp qy")
         if rd == 0:
             ts(T.d0[:], T.ne[:], 66.0, A.mult, "ne", "d0", -64.0, A.add)
-        for h in range(2):
-            op("V", lambda h=h: V.transpose(half("pv", h), bank(0, S * h + S, S * h)), "B0", "pv%d" % h)
+
+        def turned(h):
+            op("V", lambda: V.transpose(half("pv", h), bank(3 * h, S)), "B%d" % (3 * h), "pv%d" % h)
+
+        turned(0)
 
         def slot(k, t):
             return T.cmp[:, 1024 * k + t:1024 * (k + 1):4]
@@ -231,30 +237,31 @@ def rank_program(g, core, T, topo):
 
         def summed(k):
             a = C * k
-            qz(T.qc[:, a:a + C], T.sc[:, a:a + C], T.cmp[:, 4 * a:4 * (a + C)], " ".join("m%d" % (4 * k + t) for t in range(4 + (k == 3))), "qc%d" % k)
+            qz(T.qc[:, a:a + C], T.sc[:, a:a + C], T.cmp[:, 4 * a:4 * (a + C)], " ".join("m%d" % (4 * k + t) for t in range(4)), "qc%d" % k)
             mm(0, C, T.qo[:], T.so[:], T.qc[:, a:a + C], T.sc[:, a:a + C], "qo qc%d" % k, k == 0, k == 3)
 
+        cmp_v(0)
+        cmp_v(1)
+        turned(1)
         for c in range(8):
             act(slot(c // 2, c % 2 + 2), bank(2, C), "pv%d B2" % (c // 4), "m%d" % (c // 2 * 4 + c % 2 + 2), AF.Sign, scale=-1.0,
                 bias=T.pv[:, 32 * c + 16:32 * c + 17])
-        act(slot(3, 1), bank(3, C), "pv1 B3", "m13 m16", AF.Sign, scale=-1.0, bias=T.pv[:, 224:225])
-        for c in range(4):
-            cmp_v(c)
-        summed(0)
-        cmp_v(4)
-        cmp_v(5)
-        summed(1)
-        cmp_v(6)
-        summed(2)
+        for k in range(3):
+            cmp_v(2 * k + 2)
+            cmp_v(2 * k + 3)
+            summed(k)
+        summed(3)
         if rd == 0:
             scan(0, 512, T.wl[:, 0:512], "wl0 wl00", "sel")
             act(T.wn[:, 0:C], T.i8[:].indirect(L0), "i8 l", "wn0")
-        summed(3)
-        if rd == 0:
-            ts(T.off[:, 48:80], T.sel[:, 15:512:16], T.ofc[:, 0:1], A.subtract, "sel ofc", "ll", 256.0, A.mult)
+            act(T.wl[:, 2 * C:4 * C], T.wn[:, 0:C].indirect(T.off[:, 16:48]), "wn0 l", "wl1")
         for h in range(2):
+            if rd == 0 and h:
+                ts(T.off[:, 48:80], T.sel[:, 15:512:16], T.ofc[:, 0:1], A.subtract, "sel ofc", "ll", 256.0, A.mult)
             tt(half("ny", h), bank(0, S * h + S, S * h), half("i19", h), A.add, "B0 i19", "ny_%d" % h)
-            twin("k2", "ny", h)
+            if h == 0:
+                tt(half("k2", 0), bank(0, S), half("i19", 0), A.add, "B0 i19", "k2_0")
+        twin("k2", "ny", 1)
         LF, LC = T.ofe[:, 0:16], T.ofe[:, 16:24]
 
         def unpack():
@@ -275,8 +282,8 @@ def rank_program(g, core, T, topo):
             a = C * b + S * h
             tt(T.ew[:, FS * b + S * h:FS * b + S * h + S], T.fh[:, a:a + S], T.ab[:, a:a + S], A.add, "fh%d ab%d" % (b, b), "ew%d%d" % (b, h))
 
-        fill, side = {3: unpack}, {1: lambda: fetch("mc", "tt", N0, [0, 1]), 2: lambda: fetch("ny0", "ny", N0, [0, 1])}
-        for k, f in enumerate(numbers(16, LF, "lf")):
+        fill, side = {3: unpack}, {1: lambda: fetch("mc", "tt", N0, [0, 1]), 0: lambda: fetch("ny0", "ny", N0, [0, 1])}
+        for k, f in enumerate(numbers(0, LF, "lf")):
             fill[4 + k] = f
         if rd == 0:
             fill[7] = tables
@@ -294,78 +301,63 @@ def rank_program(g, core, T, topo):
         for s in range(SWEEPS):
             key = "kk" if s else "ny"
             end = s == SWEEPS - 1
-            la, lb = (N01, N02) if end else (N10, N20)
+            la, lb, lc, ld = (N01, N02, N10, N20) if s % 2 else (N10, N20, N01, N02)
             fetch("s1", key, lb, [1])
             fetch("s2", key, N0, [0, 1])
-            if rd == 0 and s == 0:
-                act(T.wl[:, 2 * C:4 * C], T.wn[:, 0:C].indirect(T.off[:, 16:48]), "wn0 l", "wl1")
             room(side, 3 * s)
             step("tt", key, la, "k2", A.min)
+            if rd == 0 and s == 0:
+                scan(512, 512, T.wl[:, 512:1024], "wl1", "sel1")
             step("tt", key, lb, "tt", A.min, [0])
             step("tt", "s1", None, "tt", A.min, [1])
             if end:
                 step("ww", "s2", None, "tt", A.is_lt)
                 break
+            if rd == 0 and s == 0:
+                ts(T.off[:, 80:112], T.sel[:, 527:1024:16], T.ofc[:, 0:1], A.subtract, "sel1 ofc", "lm", 256.0, A.mult)
             step("w0", "s2", None, "tt", A.is_lt)
             cp(half("w2", 0), half("w0", 0), "w0_0", "w2_0")
             twin("w2", "w0", 1)
-            if rd == 0 and s == 0:
-                scan(512, 512, T.wl[:, 512:1024], "wl1", "sel1")
-                ts(T.off[:, 80:112], T.sel[:, 527:1024:16], T.ofc[:, 0:1], A.subtract, "sel1 ofc", "lm", 256.0, A.mult)
-            fetch("s3", "w0", N02, [1])
+            fetch("s3", "w0", ld, [1])
             fetch("we", "w0", N0, [0, 1])
             room(side, 3 * s + 1)
             room(fill, 3 * s)
-            step("ff", "w0", N01, "w2", A.max)
-            step("ff", "w0", N02, "ff", A.max, [0])
+            step("ff", "w0", lc, "w2", A.max)
+            step("ff", "w0", ld, "ff", A.max, [0])
             step("ff", "s3", None, "ff", A.max, [1])
             step("pn", "we", None, "ff", A.subtract)
             room(fill, 3 * s + 1)
-            if s < SWEEPS - 2:
-                fetch("s4", "pn", N1, [1])
-                fetch("s5", "pn", N2, [1])
-                fetch("s5", "pn", N2, [0])
-                room(side, 3 * s + 2)
-                step("cc", "pn", N0, "ny", A.add)
-                step("cc", "pn", N1, "cc", A.add, [0])
-                step("yy", "s4", None, "s5", A.add, [1])
-                step("kk", "s5", None, "cc", A.add, [0])
-                twin("k2", "kk", 0)
-                step("kk", "yy", None, "cc", A.add, [1])
-            else:
-                fetch("s4", "pn", N20, [0, 1])
-                step("cc", "pn", N10, "ny0", A.add)
-                step("yy", "s4", None, "pn", A.add)
-                step("kk", "yy", None, "cc", A.add, [0])
-                twin("k2", "kk", 0)
-                step("kk", "yy", None, "cc", A.add, [1])
+            fetch("s4", "pn", lb, [0])
+            fetch("s4", "pn", lb, [1])
+            room(side, 3 * s + 2)
+            step("cc", "pn", la, "ny" if s % 2 else "ny0", A.add)
+            step("yy", "s4", None, "pn", A.add)
+            step("kk", "yy", None, "cc", A.add, [0])
+            twin("k2", "kk", 0)
+            step("kk", "yy", None, "cc", A.add, [1])
             twin("k2", "kk", 1)
             room(fill, 3 * s + 2)
         WW = "ww_0 ww_1 "
         op("V", lambda: V.tensor_tensor_scan(T.pp[:], T.ww[:], T.ww[:], 0.0, A.add, A.max), WW, "pp")
-        tt(T.g0[:], T.ww[:].indirect(L0), T.ny0[:], A.add, WW + "l ny0_0 ny0_1", "g0")
+        tt(T.g0[:], T.ww[:], T.ny[:], A.add, WW + "ny_0 ny_1", "g0_0 g0_1")
         for m in range(8):
             a, j = T.pp[:, 16 * m:C], T.js[:, C * m + 16 * m:C * m + C]
             if m < NV:
                 ts(j, a, T.kh[:, m:m + 1], A.is_lt, "pp kh", "js%d" % m, 2.0, A.mult)
             else:
                 act(j, a, "pp kh", "cs%d" % m, AF.Sign, scale=-1.0, bias=T.kh[:, m:m + 1], accum_out=T.cs[:, m:m + 1])
-        cp(T.g2[:], T.g0[:], "g0", "g2")
+        ts(T.ps[:], T.pp[:], U19, A.mult, "pp", "ps", -1.0, A.add)
         for m in range(NV):
             op("V", lambda m=m: V.tensor_reduce(T.cs[:, m:m + 1], T.js[:, C * m + 16 * m:C * m + C], AxisListType.X, A.add), "js%d" % m, "cs%d" % m)
-
-        def least(out, win, k, plain, r, w):
-            tt(out, win.indirect(T.off[:, 16 * k:16 * k + 16]), plain, A.min, r + " l lm", w)
-
-        least(T.mf[:], T.g0[:], N01, T.g2[:], "g0 g2", "mf")
-        act(T.ps[:], T.pp[:], "pp", "ps", AF.Identity, scale=U19, bias=-1.0)
+        tt(T.aa[:], bank(0, C), T.ps[:], A.add, "B0 ps", "aa")
+        fetch("g2", "g0", N0, [0, 1])
         tt(T.ct[:], T.cs[:], T.cor[:], A.add, "co0 co1 " + " ".join("cs%d" % m for m in range(8)), "ct")
         op("V", lambda: V.tensor_tensor_scan(T.ws2[:], T.d0[:, 0:C], T.ww[:], 0.0, A.add, A.max), WW + "d0", "ws2")
         ts(LC, T.ct[:], 0.5, A.mult, "ct", "lc")
-        tt(T.aa[:], bank(0, C), T.ps[:], A.add, "B0 ps", "aa")
+        tt(T.uu[:, S:C], T.ww[:, S:C], T.aa[:, S:C], A.mult, WW + "aa", "uu_1")
         for b in range(4):
             (cp if b < 2 else act)(T.et[:, b:4 * S:4], T.ew[:, FS * b:FS * b + C + 1].indirect(LC), "fz ew%d0 ew%d1 lc" % (b, b), "e%d" % b)
-        tt(T.uu[:, 0:S], T.ww[:, 0:S], T.aa[:, 0:S], A.mult, WW + "aa", "uu")
+        tt(T.uu[:, 0:S], T.ww[:, 0:S], T.aa[:, 0:S], A.mult, WW + "aa", "uu_0")
         qz(qe[:], se[:], T.et[:], "e0 e1 e2 e3", "qe%d" % rd)
 
         def send(qe=qe, se=se, ql=ql, sl=sl, rd=rd):
@@ -373,54 +365,54 @@ def rank_program(g, core, T, topo):
             g.remote_dma(sl[:], se[:], T.sem["arr%d" % rd], T.sem.sent, pid, rid, mask)
 
         op("G", send, "qe%d" % rd, "")
-        tt(T.uu[:, S:C], T.ww[:, S:C], T.aa[:, S:C], A.mult, WW + "aa", "uv")
-        act(T.u2[:], T.uu[:], "uu uv", "u2")
+        ts(T.ow1[:], T.ws2[:, 15:C:16], -1.0, A.mult, "ws2 ofe", "ow1", T.ofc[:, 2:3], A.add)
+        fetch("mc", "g0", N1, [0, 1])
+        fetch("s1", "uu", N0, [0, 1])
+        fetch("s2", "uu", N1, [0, 1])
         if rd == R - 1:
             act(T.cw[:, 1:S + 1], T.iot[:].indirect(LC), "iot lc", "cw")
-        ts(T.ow1[:], T.ws2[:, 15:C:16], -1.0, A.mult, "ws2 ofe", "ow1", T.ofc[:, 2:3], A.add)
-        least(T.mf[:], T.g0[:], N02, T.mf[:], "g0 mf", "mf")
+        tt(T.mf[:], T.g0[:].indirect(T.off[:, 32:48]), T.g2[:], A.min, "g0_0 g0_1 g2_0 g2_1 l", "mf")
         tt(T.ow2[:], T.ow1[:], T.own[:], A.add, "own ow1", "ow2")
-        least(T.mq[:], T.uu[:], N0, T.u2[:], "uu uv u2", "ms")
+        tt(T.mf[:], T.mc[:], T.mf[:], A.min, "mc_0 mc_1 mf", "mf")
+        LS, LQ = T.oft[:, 0:16], T.oft[:, 16:32]
+        step("mq", "uu", N2, "s1", A.min)
+        step("mq", "s2", None, "mq", A.min)
+        step("mq", "uu", None, "mq", A.min)
         scan(C, C, T.mf[:], "mf", "sel1")
-        least(T.mq[:], T.uu[:], N1, T.mq[:], "uu ms", "ms")
+        scan(0, C, T.mq[:], "mq_0 mq_1", "sel")
         tt(T.sel[:, C + 15:2 * C:16], T.sel[:, C + 15:2 * C:16], T.ow2[:], A.min, "sel1 ow2", "sel1")
         if rd == 0:
             qz(T.qv[:], T.sv[:], T.vt[:], "vt", "qv")
-        least(T.mq[:], T.uu[:], N2, T.mq[:], "uu ms", "ms")
-        scan(0, C, T.mq[:], "ms", "sel")
-        for f in numbers(32, T.oft[:], "lt"):
+        for f, h in zip(numbers(0, LS, "ls"), numbers(1, LQ, "lq")):
             f()
-        LS, LQ = T.oft[:, 0:16], T.oft[:, 16:32]
+            h()
         op("T", lambda rd=rd: PE.wait_ge(T.sem["arr%d" % rd], 2 * nin), "", "")
         for b in range(4):
             mm(b, S, T.qw[:, 128 * b:128 * b + 128], T.sw[:, 128 * b:128 * b + 128], ql[:], sl[:], "qw")
-        for b in range(5):
-            if b < 4:
+        for b in range(4):
+            if b % 2:
                 act(T.hh[:, HS * b + 1:HS * b + S + 1], bank(b, S), "B%d" % b, "hh%d" % b, scale=2.0 ** -6)
-            if b:
-                act(T.g1[:, C * b - C:C * b], T.hh[:, HS * b - HS:HS * b - HS + S + 1].indirect(LS), "hz hh%d lt" % (b - 1), "g1%d" % (b - 1))
-        act(T.g3[:, 3 * C:4 * C], T.g1[:, 3 * C:4 * C], "g13", "g33")
-        cp(T.g3[:, 0:C], T.hh[:, 0:S + 1].indirect(LS), "hz hh0 lt", "g30")
+            else:
+                ts(T.hh[:, HS * b + 1:HS * b + S + 1], bank(b, S), 2.0 ** -6, A.mult, "B%d" % b, "hh%d" % b)
+        for b in range(4):
+            (act if b == 1 else cp)(T.g1[:, C * b:C * (b + 1)], T.hh[:, HS * b:HS * b + S + 1].indirect(LS), "hz hh%d ls" % b, "g1%d" % b)
+        for b in range(4):
+            act(T.g3[:, C * b:C * (b + 1)], T.g1[:, C * b:C * (b + 1)].indirect(LQ), "g1%d lq" % b, "g3%d" % b)
         if rd == R - 1:
-            act(T.pw[:], T.cw[:, 0:S + 1].indirect(LS), "cz cw lt", "pw")
+            act(T.pw[:], T.cw[:, 0:S + 1].indirect(LS), "cz cw ls", "pw")
             dma("Y", [(T.op[k:k + 1, :], T.pw[16 * k:16 * k + 1, :]) for k in range(8)], "pw", "out0")
 
         def added(b):
-            tt(T.tb[:, C * b:C * (b + 1)], T.g1[:, C * b:C * (b + 1)].indirect(LQ), T.g3[:, C * b:C * (b + 1)], A.add, "g1%d g3%d lt" % (b, b), "tb%d" % b)
+            tt(T.tb[:, C * b:C * (b + 1)], T.g1[:, C * b:C * (b + 1)], T.g3[:, C * b:C * (b + 1)], A.add, "g1%d g3%d" % (b, b), "tb%d" % b)
 
         def state(b, a=0, e=C):
             tt(T.xt[:, 4 * a + b:4 * e:4], T.tb[:, C * b + a:C * b + e], bank(4 + b, e, a), A.add, "tb%d B%d" % (b, 4 + b), "x%d" % (b + (a > 0)))
 
-        def again(b):
-            cp(T.g3[:, C * b:C * (b + 1)], T.g1[:, C * b:C * (b + 1)], "g1%d" % b, "g3%d" % b)
-
         added(0)
-        again(1)
-        state(0)
         added(1)
-        again(2)
-        state(1)
+        state(0)
         added(2)
+        state(1)
         added(3)
         state(2)
         state(3, 0, S)

from concourse.mybir import dt, AluOpType as A, AxisListType, ActivationFunctionType as AF

C, S, R, SWEEPS = 256, 128, 3, 8
NV = 2
FS, HS = 272, 144
U19 = 2.0 ** -19
F32, B16, I32, U16, X4, U8 = "float32", "bfloat16", "int32", "uint16", "float8_e4m3fn_x4", "uint8"


def _sb(n, d):
    return ("sbuf", [128, n], d)


SCRATCH = {
    "xt": _sb(4 * C, B16), "ut": _sb(512, B16), "vt": _sb(512, B16), "ni": _sb(48, I32),
    "qx": _sb(C, X4), "sx": _sb(C, U8), "qu": _sb(128, X4), "su": _sb(128, U8), "qv": _sb(128, X4), "sv": _sb(128, U8),
    "qp": _sb(384, X4), "sp": _sb(384, U8), "qw": _sb(512, X4), "sw": _sb(512, U8),
    "ot": _sb(512, B16), "qo": _sb(128, X4), "so": _sb(128, U8),
    "idt": _sb(2048, B16), "qi": _sb(512, X4), "si": _sb(512, U8),
    "cmp": _sb(4096, B16), "qc": _sb(1024, X4), "sc": _sb(1024, U8),
    "iot": _sb(264, F32), "i19": _sb(C, F32), "i8": _sb(C, F32), "jm": _sb(512, B16),
    "ne": _sb(512, B16), "d0": _sb(512, B16), "pi": _sb(2, I32), "pj": _sb(2, I32), "pm": _sb(2, F32), "ofc": _sb(4, F32),
    "kh": _sb(8, B16), "cor": _sb(8, F32), "uli": _sb(24, I32), "ulo": _sb(24, U16),
    "off": _sb(112, U16), "wn": _sb(768, F32), "wl": _sb(1024, F32), "sel": _sb(1024, F32),
    "pv": _sb(C, F32), "ny": _sb(C, F32), "ny0": _sb(C, F32), "we": _sb(C, B16), "kk": _sb(C, F32), "k2": _sb(C, F32),
    "tt": _sb(C, F32), "w0": _sb(C, B16), "w2": _sb(C, B16), "ff": _sb(C, B16), "pn": _sb(C, B16), "cc": _sb(C, F32),
    "s1": _sb(C, F32), "s2": _sb(C, F32), "s3": _sb(C, B16), "s4": _sb(C, B16), "yy": _sb(C, B16),
    "ww": _sb(C, B16), "pp": _sb(C, B16), "g2": _sb(C, F32), "g3": _sb(4 * C, B16), "own": _sb(16, F32),
    "js": _sb(8 * C, B16), "cs": _sb(8, F32), "ct": _sb(8, F32), "ofe": _sb(24, U16),
    "g0": _sb(C, F32), "mf": _sb(C, F32), "mc": _sb(C, F32), "na": _sb(32, I32), "nb": _sb(32, I32),
    "ps": _sb(C, F32), "aa": _sb(C, F32), "uu": _sb(C, F32), "mq": _sb(C, F32), "oft": _sb(32, U16),
    "ws2": _sb(C, B16), "ow1": _sb(16, F32), "ow2": _sb(16, F32),
    "fh": _sb(4 * C, B16), "ab": _sb(4 * C, B16), "ew": _sb(4 * FS, B16), "et": _sb(512, B16), "hh": _sb(4 * HS, B16),
    "g1": _sb(4 * C, B16), "tb": _sb(4 * C, B16), "cw": _sb(HS, F32), "pw": _sb(C, F32), "yt": _sb(C, F32),
    "pa": ("psum", [128, 4096], F32),
}
for _r in range(R):
    SCRATCH["qe%d" % _r] = _sb(S, X4)
    SCRATCH["se%d" % _r] = _sb(S, U8)
    SCRATCH["ql%d" % _r] = _sb(S, X4)
    SCRATCH["sl%d" % _r] = _sb(S, U8)
NCS, NDS = 60, 24
SEMAPHORES = ["c%d" % i for i in range(NCS)] + ["d%d" % i for i in range(NDS)] + ["arr%d" % i for i in range(R)] + ["sent"]


def emit(g, T, ops):
    queue = {"V": g.vector, "S": g.scalar, "T": g.tensor, "G": g, "Y": g.sync}
    wr, rd, know, done, waits = {}, {}, {q: 0 for q in queue}, [], []
    for i, o in enumerate(ops):
        q, dep = o["q"], set()
        for k in o["r"]:
            if k in wr:
                dep.add(wr[k])
            if k[0] == "B":
                dep.update(j for j in rd.get(k, []) if ops[j]["q"] != q)
        for k in o["w"]:
            if k in wr and not (o["acc"] and ops[wr[k]]["q"] == q):
                dep.add(wr[k])
            dep.update(rd.get(k, []))
        need = []
        for j in sorted(dep, reverse=True):
            if not know[q] >> j & 1:
                need.append(j)
                know[q] |= done[j]
        waits.append(need)
        o["known"] = know[q]
        done.append(know[q] | 1 << i)
        for k in o["r"]:
            rd.setdefault(k, []).append(i)
        for k in o["w"]:
            wr[k] = i
            rd[k] = []
    signals = set(j for w in waits for j in w)
    last, count, where, nd = [None] * NCS, [0] * NCS, {}, [0]
    for i, o in enumerate(ops):
        eng = queue[o["q"]]
        for j in waits[i]:
            eng.wait_ge(T.sem[where[j][0]], where[j][1])
        ins = o["f"]()
        if i not in signals:
            continue
        if o["dma"]:
            name = "d%d" % nd[0]
            nd[0] += 1
            for x in ins:
                x.then_inc(T.sem[name], 16)
            where[i] = (name, 16 * len(ins))
        else:
            s = [k for k in range(NCS) if last[k] is None or o["known"] >> last[k] & 1][0]
            last[s] = i
            count[s] += 1
            ins.then_inc(T.sem["c%d" % s], 1)
            where[i] = ("c%d" % s, count[s])


def rank_program(g, core, T, topo):
    rank = T.rank_of(core)
    if rank is None:
        return
    nxt = T.cores[(rank + 1) % len(T.cores)]
    rid, pid = topo.addr(nxt)[:2]
    mask, nout = topo.mask(core, nxt), len(topo.engines(core, nxt))
    nin = len(topo.engines(T.cores[rank - 1], core))
    V, SC, PE = g.vector, g.scalar, g.tensor
    ops = []

    def op(q, f, r, w, dma=False, acc=False):
        ops.append({"q": q, "f": f, "r": r.split(), "w": w.split(), "dma": dma, "acc": acc})

    def tt(out, a, b, o, r, w):
        op("V", lambda: V.tensor_tensor(out, a, b, o), r, w)

    def ts(out, a, s1, o0, r, w, s2=None, o1=None):
        if o1 is None:
            op("V", lambda: V.tensor_scalar(out, a, s1, None, o0), r, w)
        else:
            op("V", lambda: V.tensor_scalar(out, a, s1, s2, o0, o1), r, w)

    def cp(out, a, r, w):
        op("V", lambda: V.tensor_copy(out, a), r, w)

    def ms(out, c, w):
        op("V", lambda: V.memset(out, c), "", w)

    def act(out, a, r, w, f=AF.Copy, **kw):
        op("S", lambda: SC.activation(out, a, f, **kw), r, w)

    def qz(q, s, a, r, w):
        op("V", lambda: V.quantize_mx(q, s, a), r, w)

    def bank(b, n, a=0):
        return T.pa[:, 512 * b + a:512 * b + n]

    def mm(b, n, lq, ls, rq, rs, r, start=True, stop=True):
        op("T", lambda: PE.matmul_mx(bank(b, n), lq, ls, rq, rs, start, stop), r, "B%d" % b, acc=not start)

    def dma(q, pairs, r, w):
        e = {"Y": g.sync, "S": SC}[q]
        op(q, lambda: [e.dma_start(a, b) for a, b in pairs], r, w, dma=True)

    def iota(out, pat, base, mul, w, flt=True):
        if flt:
            op("G", lambda: g.iota(out, pat, base, mul, allow_small_or_imprecise_dtypes=True), "", w)
        else:
            op("G", lambda: g.iota(out, pat, base, mul), "", w)

    def scan(a, n, src, r, w):
        op("V", lambda: V.tensor_tensor_scan(T.sel[:, a:a + n], T.d0[:, 0:n], src, 0.0, A.add, A.max), r + " d0", w)

    def numbers(k, out, w):
        na, nb = T.na[:, 16 * k:16 * k + 16], T.nb[:, 16 * k:16 * k + 16]
        return [lambda: ts(na, T.sel[:, C * k + 15:C * k + C:16], 1.0 / U19, A.mult, ("sel", "sel1")[k], "na%d" % k),
                lambda: ts(nb, na, 511, A.bitwise_and, "na%d" % k, "nb%d" % k),
                lambda: cp(out, nb, "nb%d" % k, w)]

    N0, N1, N2, N10, N20, N01, N02 = range(7)
    L0 = T.off[:, 0:16]

    dma("S", [(T.ni[:, 0:16], T.n0[:]), (T.ni[:, 16:32], T.n1[:]), (T.ni[:, 32:48], T.n2[:])], "", "ni")
    dma("Y", [(T.ut[:], T.u[:])], "", "ut")
    dma("Y", [(T.xt[:], T.x[:])], "", "x0 x1 x2 x3 x4")
    dma("Y", [(T.qw[:].bitcast(dt.uint8), T.wc[:]), (T.sw[:], T.ws[:])], "", "qw")
    dma("Y", [(T.vt[:], T.v[:])], "", "vt")
    iota(T.pi[:, 0:1], [[0, 1]], 0, 1, "pi", False)
    iota(T.iot[:], [[1, 264]], 0, 0, "iot")
    iota(T.uli[:, 0:8], [[16, 8]], 0, 0, "ul0", False)
    iota(T.uli[:, 8:24], [[16, 2], [32, 4], [0, 2]], 0, 0, "ul1", False)
    iota(T.jm[:], [[0, 32], [1, 16]], 0, 0, "jm")
    iota(T.idt[:], [[0, 2048]], 1, 0, "idt")
    op("G", lambda: g.affine_select(T.idt[:], T.idt[:], [[-1, 4], [-8, 128], [1, 4]], A.is_equal, 0.0, 0, 8), "idt", "idt")
    ms(T.ot[:], 0.0, " ".join("o%d" % k for k in range(16)))
    for b in range(4):
        for t in range(4):
            a = 4 * (32 * b + 16 * (t // 2)) + t
            ms(T.ot[32 * b:32 * b + 32, a:a + 61:4], 2.0 ** -10, "o%d" % (4 * b + t))
    ms(T.ew[:, C:4 * FS:FS], 0.0, "fz")
    ms(T.hh[:, 0:4 * HS:HS], 0.0, "hz")
    ts(T.pj[:, 0:1], T.pi[:, 0:1], 15, A.bitwise_and, "pi", "pj")
    ms(T.cw[:, 0:1], -1.0, "cz")
    cp(T.pm[:, 0:1], T.pj[:, 0:1], "pj", "pm")
    qz(T.qo[:], T.so[:], T.ot[:], " ".join("o%d" % k for k in range(16)), "qo")
    act(T.i8[:], T.iot[:, 0:C], "iot", "i8", scale=2.0 ** -8)
    act(T.i19[:], T.iot[:, 0:C], "iot", "i19", scale=U19)
    cp(T.ulo[:], T.uli[:], "ul0 ul1", "ulo")
    cp(T.off[:, 0:48], T.ni[:], "ni", "l")
    act(T.wn[:, C:3 * C], T.i8[:].indirect(T.off[:, 16:48]), "i8 l", "wn")
    ts(T.ofc[:, 0:1], T.pm[:, 0:1], -2.0, A.mult, "pm", "ofc", 30.0, A.add)
    ts(T.ne[:], T.jm[:], T.pm[:, 0:1], A.not_equal, "jm pm", "ne")
    qz(T.qu[:], T.su[:], T.ut[:], "ut", "qu")
    cp(T.qp[:].bitcast(dt.uint32), T.qu[:].bitcast(dt.uint32).indirect(T.ulo[:]), "qu ulo", "qp")
    act(T.sp[:], T.su[:].indirect(T.ulo[:]), "qu ulo", "sp")
    act(T.wl[:, 0:C], T.wn[:, C:2 * C].indirect(L0), "wn l", "wl0")
    act(T.wl[:, C:2 * C], T.wn[:, 2 * C:3 * C].indirect(L0), "wn l", "wl00")

    def packed():
        qz(T.qx[:, 0:S], T.sx[:, 0:S], T.xt[:, 0:4 * S], "x0 x1 x2 x3", "qx")
        qz(T.qx[:, S:C], T.sx[:, S:C], T.xt[:, 4 * S:4 * C], "x0 x1 x2 x4", "qy")

    def half(n, h):
        return T[n][:, S * h:S * h + S]

    def picked(win, k, hs):
        return T[win][:].indirect(T.off[:, 16 * k + 8 * hs[0]:16 * k + 8 * hs[-1] + 8]), "l %s %s_0 %s_1" % ("lm" if k in (N01, N02) else "ll", win, win)

    def step(out, win, k, plain, o, hs=(0, 1)):
        for h in hs:
            a, r = (half(win, h), "%s_%d" % (win, h)) if k is None else picked(win, k, [h])
            tt(half(out, h), a, half(plain, h), o, "%s %s_%d" % (r, plain, h), "%s_%d" % (out, h))

    def fetch(out, win, k, hs):
        a, r = picked(win, k, hs)
        act(T[out][:, S * hs[0]:S * hs[-1] + S], a, r, " ".join("%s_%d" % (out, h) for h in hs))

    def twin(out, src, h):
        act(half(out, h), half(src, h), "%s_%d" % (src, h), "%s_%d" % (out, h))

    for rd in range(R):
        qe, se, ql, sl = [T[n + str(rd)] for n in ("qe", "se", "ql", "sl")]
        packed()
        mm(0, S, T.qp[:, 0:128], T.sp[:, 0:128], T.qx[:, 0:S], T.sx[:, 0:S], "qp sp qx")
        for b in (1, 2):
            mm(b, C, T.qp[:, 128 * b:128 * b + 128], T.sp[:, 128 * b:128 * b + 128], T.qx[:], T.sx[:], "qp sp qx qy")
        mm(3, S, T.qp[:, 0:128], T.sp[:, 0:128], T.qx[:, S:C], T.sx[:, S:C], "qp sp qy")
        if rd == 0:
            ts(T.d0[:], T.ne[:], 66.0, A.mult, "ne", "d0", -64.0, A.add)

        def turned(h):
            op("V", lambda: V.transpose(half("pv", h), bank(3 * h, S)), "B%d" % (3 * h), "pv%d" % h)

        turned(0)

        def slot(k, t):
            return T.cmp[:, 1024 * k + t:1024 * (k + 1):4]

        def cmp_v(c):
            ts(slot(c // 2, c % 2), bank(1, C), T.pv[:, 32 * c:32 * c + 1], A.is_lt, "B1 pv%d" % (c // 4), "m%d" % (c // 2 * 4 + c % 2))

        def summed(k):
            a = C * k
            qz(T.qc[:, a:a + C], T.sc[:, a:a + C], T.cmp[:, 4 * a:4 * (a + C)], " ".join("m%d" % (4 * k + t) for t in range(4)), "qc%d" % k)
            mm(0, C, T.qo[:], T.so[:], T.qc[:, a:a + C], T.sc[:, a:a + C], "qo qc%d" % k, k == 0, k == 3)

        cmp_v(0)
        cmp_v(1)
        turned(1)
        for c in range(8):
            act(slot(c // 2, c % 2 + 2), bank(2, C), "pv%d B2" % (c // 4), "m%d" % (c // 2 * 4 + c % 2 + 2), AF.Sign, scale=-1.0,
                bias=T.pv[:, 32 * c + 16:32 * c + 17])
        for k in range(3):
            cmp_v(2 * k + 2)
            cmp_v(2 * k + 3)
            summed(k)
        summed(3)
        if rd == 0:
            scan(0, 512, T.wl[:, 0:512], "wl0 wl00", "sel")
            act(T.wn[:, 0:C], T.i8[:].indirect(L0), "i8 l", "wn0")
            act(T.wl[:, 2 * C:4 * C], T.wn[:, 0:C].indirect(T.off[:, 16:48]), "wn0 l", "wl1")
        for h in range(2):
            if rd == 0 and h:
                ts(T.off[:, 48:80], T.sel[:, 15:512:16], T.ofc[:, 0:1], A.subtract, "sel ofc", "ll", 256.0, A.mult)
            tt(half("ny", h), bank(0, S * h + S, S * h), half("i19", h), A.add, "B0 i19", "ny_%d" % h)
            if h == 0:
                tt(half("k2", 0), bank(0, S), half("i19", 0), A.add, "B0 i19", "k2_0")
        twin("k2", "ny", 1)
        LF, LC = T.ofe[:, 0:16], T.ofe[:, 16:24]

        def unpack():
            if rd == 0:
                qz(T.qi[:], T.si[:], T.idt[:], "idt", "qi")
            for b in range(4):
                mm(4 + b, C, T.qi[:, 128 * b:128 * b + 128], T.si[:, 128 * b:128 * b + 128], T.qx[:], T.sx[:], "qi qx qy")
            scan(0, C, T.mc[:], "mc_0 mc_1", "sel")

        def tables():
            ts(T.kh[:], T.iot[:, 0:128:16], T.pm[:, 0:1], A.add, "iot pm", "kh", 0.5, A.add)
            ts(T.cor[:, 0:NV], T.iot[:, 0:16 * NV:16], 2.0, A.mult, "iot", "co0")
            ts(T.cor[:, NV:8], T.iot[:, 16 * NV:128:16], 256.0, A.add, "iot", "co1")
            ts(T.ofc[:, 1:2], T.pm[:, 0:1], U19, A.mult, "pm", "ofd", 0.5, A.add)
            ts(T.ofc[:, 2:3], T.pm[:, 0:1], -4.0, A.mult, "pm", "ofe", 60.0, A.add)

        def mean(b, h):
            a = C * b + S * h
            tt(T.ew[:, FS * b + S * h:FS * b + S * h + S], T.fh[:, a:a + S], T.ab[:, a:a + S], A.add, "fh%d ab%d" % (b, b), "ew%d%d" % (b, h))

        fill, side = {3: unpack}, {1: lambda: fetch("mc", "tt", N0, [0, 1]), 0: lambda: fetch("ny0", "ny", N0, [0, 1])}
        for k, f in enumerate(numbers(0, LF, "lf")):
            fill[4 + k] = f
        if rd == 0:
            fill[7] = tables
            fill[8] = lambda: ts(T.own[:], T.iot[:, 0:C:16], U19, A.mult, "iot ofd", "own", T.ofc[:, 1:2], A.add)
        for b in range(4):
            side[5 + b] = lambda b=b: act(T.fh[:, C * b:C * b + C], bank(4 + b, C), "B%d" % (4 + b), "fh%d" % b, scale=0.5)
            side[9 + b] = lambda b=b: act(T.ab[:, C * b:C * b + C], T.fh[:, C * b:C * b + C].indirect(LF), "fh%d lf" % b, "ab%d" % b)
        for k in range(8):
            fill[13 + k] = lambda k=k: mean(k // 2, k % 2)

        def room(table, k):
            if k in table:
                table[k]()

        for s in range(SWEEPS):
            key = "kk" if s else "ny"
            end = s == SWEEPS - 1
            la, lb, lc, ld = (N01, N02, N10, N20) if s % 2 else (N10, N20, N01, N02)
            fetch("s1", key, lb, [1])
            fetch("s2", key, N0, [0, 1])
            room(side, 3 * s)
            step("tt", key, la, "k2", A.min)
            if rd == 0 and s == 0:
                scan(512, 512, T.wl[:, 512:1024], "wl1", "sel1")
            step("tt", key, lb, "tt", A.min, [0])
            step("tt", "s1", None, "tt", A.min, [1])
            if end:
                step("ww", "s2", None, "tt", A.is_lt)
                break
            if rd == 0 and s == 0:
                ts(T.off[:, 80:112], T.sel[:, 527:1024:16], T.ofc[:, 0:1], A.subtract, "sel1 ofc", "lm", 256.0, A.mult)
            step("w0", "s2", None, "tt", A.is_lt)
            cp(half("w2", 0), half("w0", 0), "w0_0", "w2_0")
            twin("w2", "w0", 1)
            fetch("s3", "w0", ld, [1])
            fetch("we", "w0", N0, [0, 1])
            room(side, 3 * s + 1)
            room(fill, 3 * s)
            step("ff", "w0", lc, "w2", A.max)
            step("ff", "w0", ld, "ff", A.max, [0])
            step("ff", "s3", None, "ff", A.max, [1])
            step("pn", "we", None, "ff", A.subtract)
            room(fill, 3 * s + 1)
            fetch("s4", "pn", lb, [0])
            fetch("s4", "pn", lb, [1])
            room(side, 3 * s + 2)
            step("cc", "pn", la, "ny" if s % 2 else "ny0", A.add)
            step("yy", "s4", None, "pn", A.add)
            step("kk", "yy", None, "cc", A.add, [0])
            twin("k2", "kk", 0)
            step("kk", "yy", None, "cc", A.add, [1])
            twin("k2", "kk", 1)
            room(fill, 3 * s + 2)
        WW = "ww_0 ww_1 "
        op("V", lambda: V.tensor_tensor_scan(T.pp[:], T.ww[:], T.ww[:], 0.0, A.add, A.max), WW, "pp")
        tt(T.g0[:], T.ww[:], T.ny[:], A.add, WW + "ny_0 ny_1", "g0_0 g0_1")
        for m in range(8):
            a, j = T.pp[:, 16 * m:C], T.js[:, C * m + 16 * m:C * m + C]
            if m < NV:
                ts(j, a, T.kh[:, m:m + 1], A.is_lt, "pp kh", "js%d" % m, 2.0, A.mult)
            else:
                act(j, a, "pp kh", "cs%d" % m, AF.Sign, scale=-1.0, bias=T.kh[:, m:m + 1], accum_out=T.cs[:, m:m + 1])
        ts(T.ps[:], T.pp[:], U19, A.mult, "pp", "ps", -1.0, A.add)
        for m in range(NV):
            op("V", lambda m=m: V.tensor_reduce(T.cs[:, m:m + 1], T.js[:, C * m + 16 * m:C * m + C], AxisListType.X, A.add), "js%d" % m, "cs%d" % m)
        tt(T.aa[:], bank(0, C), T.ps[:], A.add, "B0 ps", "aa")
        fetch("g2", "g0", N0, [0, 1])
        tt(T.ct[:], T.cs[:], T.cor[:], A.add, "co0 co1 " + " ".join("cs%d" % m for m in range(8)), "ct")
        op("V", lambda: V.tensor_tensor_scan(T.ws2[:], T.d0[:, 0:C], T.ww[:], 0.0, A.add, A.max), WW + "d0", "ws2")
        ts(LC, T.ct[:], 0.5, A.mult, "ct", "lc")
        tt(T.uu[:, S:C], T.ww[:, S:C], T.aa[:, S:C], A.mult, WW + "aa", "uu_1")
        for b in range(4):
            (cp if b < 2 else act)(T.et[:, b:4 * S:4], T.ew[:, FS * b:FS * b + C + 1].indirect(LC), "fz ew%d0 ew%d1 lc" % (b, b), "e%d" % b)
        tt(T.uu[:, 0:S], T.ww[:, 0:S], T.aa[:, 0:S], A.mult, WW + "aa", "uu_0")
        qz(qe[:], se[:], T.et[:], "e0 e1 e2 e3", "qe%d" % rd)

        def send(qe=qe, se=se, ql=ql, sl=sl, rd=rd):
            g.remote_dma(ql[:].bitcast(dt.uint8), qe[:].bitcast(dt.uint8), T.sem["arr%d" % rd], T.sem.sent, pid, rid, mask)
            g.remote_dma(sl[:], se[:], T.sem["arr%d" % rd], T.sem.sent, pid, rid, mask)

        op("G", send, "qe%d" % rd, "")
        ts(T.ow1[:], T.ws2[:, 15:C:16], -1.0, A.mult, "ws2 ofe", "ow1", T.ofc[:, 2:3], A.add)
        fetch("mc", "g0", N1, [0, 1])
        fetch("s1", "uu", N0, [0, 1])
        fetch("s2", "uu", N1, [0, 1])
        if rd == R - 1:
            act(T.cw[:, 1:S + 1], T.iot[:].indirect(LC), "iot lc", "cw")
        tt(T.mf[:], T.g0[:].indirect(T.off[:, 32:48]), T.g2[:], A.min, "g0_0 g0_1 g2_0 g2_1 l", "mf")
        tt(T.ow2[:], T.ow1[:], T.own[:], A.add, "own ow1", "ow2")
        tt(T.mf[:], T.mc[:], T.mf[:], A.min, "mc_0 mc_1 mf", "mf")
        LS, LQ = T.oft[:, 0:16], T.oft[:, 16:32]
        step("mq", "uu", N2, "s1", A.min)
        step("mq", "s2", None, "mq", A.min)
        step("mq", "uu", None, "mq", A.min)
        scan(C, C, T.mf[:], "mf", "sel1")
        scan(0, C, T.mq[:], "mq_0 mq_1", "sel")
        tt(T.sel[:, C + 15:2 * C:16], T.sel[:, C + 15:2 * C:16], T.ow2[:], A.min, "sel1 ow2", "sel1")
        if rd == 0:
            qz(T.qv[:], T.sv[:], T.vt[:], "vt", "qv")
        for f, h in zip(numbers(0, LS, "ls"), numbers(1, LQ, "lq")):
            f()
            h()
        op("T", lambda rd=rd: PE.wait_ge(T.sem["arr%d" % rd], 2 * nin), "", "")
        for b in range(4):
            mm(b, S, T.qw[:, 128 * b:128 * b + 128], T.sw[:, 128 * b:128 * b + 128], ql[:], sl[:], "qw")
        for b in range(4):
            if b % 2:
                act(T.hh[:, HS * b + 1:HS * b + S + 1], bank(b, S), "B%d" % b, "hh%d" % b, scale=2.0 ** -6)
            else:
                ts(T.hh[:, HS * b + 1:HS * b + S + 1], bank(b, S), 2.0 ** -6, A.mult, "B%d" % b, "hh%d" % b)
        for b in range(4):
            (act if b == 1 else cp)(T.g1[:, C * b:C * (b + 1)], T.hh[:, HS * b:HS * b + S + 1].indirect(LS), "hz hh%d ls" % b, "g1%d" % b)
        for b in range(4):
            act(T.g3[:, C * b:C * (b + 1)], T.g1[:, C * b:C * (b + 1)].indirect(LQ), "g1%d lq" % b, "g3%d" % b)
        if rd == R - 1:
            act(T.pw[:], T.cw[:, 0:S + 1].indirect(LS), "cz cw ls", "pw")
            dma("Y", [(T.op[k:k + 1, :], T.pw[16 * k:16 * k + 1, :]) for k in range(8)], "pw", "out0")

        def added(b):
            tt(T.tb[:, C * b:C * (b + 1)], T.g1[:, C * b:C * (b + 1)], T.g3[:, C * b:C * (b + 1)], A.add, "g1%d g3%d" % (b, b), "tb%d" % b)

        def state(b, a=0, e=C):
            tt(T.xt[:, 4 * a + b:4 * e:4], T.tb[:, C * b + a:C * b + e], bank(4 + b, e, a), A.add, "tb%d B%d" % (b, 4 + b), "x%d" % (b + (a > 0)))

        added(0)
        added(1)
        state(0)
        added(2)
        state(1)
        added(3)
        state(2)
        state(3, 0, S)
        state(3, S, C)
    packed()
    mm(0, C, T.qv[:], T.sv[:], T.qx[:], T.sx[:], "qv qx qy")
    dma("Y", [(T.oc[:], T.qx[:].bitcast(dt.uint8))], "qx qy", "out1")
    dma("S", [(T.osc[4 * k:4 * k + 4, :], T.sx[32 * k:32 * k + 4, :]) for k in range(4)], "qx qy", "out2")
    cp(T.yt[:], bank(0, C), "B0", "yt")
    dma("Y", [(T.y[:], T.yt[:])], "yt", "out3")
    op("G", lambda: g.wait_ge(T.sem.sent, 2 * R * nout), "out0 out1 out2 out3", "")
    emit(g, T, ops)
